import numpy as np, ml_dtypes
CORES = [242,247,114,119]
N = 4
BF = ml_dtypes.bfloat16
def gentries(a):
    return np.ascontiguousarray(a.reshape(8, 16, -1).transpose(0, 2, 1)).reshape(8, -1)
def gtable(e):
    e = np.asarray(e); return np.ascontiguousarray(e.reshape(8, -1, 16).transpose(0, 2, 1)).reshape(128, -1).astype(np.int32)
S, M, NA, RO = 128, 512, 1024, 4
W0 = M + (N - 1) * S; W = W0 + RO * S
def parts(rng):
    amp = rng.choice(np.array([255, 160, 96]), (1, 8, 1, 1))
    y = (rng.random((N, 8, 16, W0)) * (amp + 1)).astype(np.int64)
    l = rng.integers(0, W0, (N, 8, 16, NA)); c = rng.integers(0, NA, (N, 8, 16, M))
    f = np.where(rng.random((N, 8, W0)) < 0.3, rng.integers(0, W0, (N, 8, W0)), np.arange(W0))
    th = (amp[..., 0] * (4.6 + 2.2 * rng.random((N, 8, S)))).astype(np.int64)
    return y, l, c, f, th
def pack(y, l, c, f, th):
    return {"y0": np.ascontiguousarray(y.reshape(N, 128, W0)).astype(np.float32).astype(BF), "lk": np.ascontiguousarray(l.reshape(N, 128, NA)).astype(np.int32),
            "cl": np.ascontiguousarray(c.reshape(N, 128, M)).astype(np.int32), "fw0": np.stack([gtable(z) for z in f]), "th": np.ascontiguousarray(th).astype(np.int32)}
def uneven(rng, hi, *shape):
    z = rng.random(shape) ** 3; side = rng.random(shape[:2] + (1,) * (len(shape) - 2)) < 0.5
    return np.minimum((hi * np.where(side, z, 1 - z)).astype(np.int64), hi - 1)
def far(y, l, c, f):
    r4 = np.arange(N)[:, None, None, None]; g4 = np.arange(8)[None, :, None, None]; k4 = np.arange(16)[None, None, :, None]
    a = c[..., :S]; b = f[r4, g4, l[r4, g4, k4, a]].reshape(N, 8, 1, 16 * S); e = f[r4, g4, l[r4, g4, (k4 + 5) % 16, a]].reshape(N, 8, 1, 16 * S)
    z = ((np.take_along_axis(y, b, 3) + np.take_along_axis(y, e, 3)) >> 1).reshape(N, 8, 16, 16, S)
    return np.max(np.add.reduce(np.abs(z - y[..., :S][:, :, :, None, :]), axis=2), axis=2)
def setup_inputs(rng):
    return pack(*parts(rng))
def setup_inputs_spread(rng):
    y, l, c, f, th = parts(rng)
    y = np.minimum((np.exp2(8 * rng.random((N, 8, 1, W0))) * rng.random((N, 8, 16, W0))).astype(np.int64), 255)
    l = uneven(rng, W0, N, 8, 16, NA); c = uneven(rng, NA, N, 8, 16, M)
    f = np.where(rng.random((N, 8, W0)) < 0.5, uneven(rng, W0, N, 8, W0), f)
    th = np.minimum((4081 * rng.random((N, 8, S)) ** 3).astype(np.int64), 4080)
    return pack(y, l, c, f, th)
def setup_inputs_ends(rng):
    y, l, c, f, th = parts(rng)
    y = np.where(rng.random((N, 8, 1, W0)) < 0.6, 255 * rng.integers(0, 2, (N, 8, 1, W0)), 255 * rng.integers(0, 2, (N, 8, 16, W0)))
    y[..., 0] = 0; y[..., W0 - 1] = 255; y[..., S - 1] = 0
    l = np.where(rng.random(l.shape) < 0.72, (W0 - 1) * rng.integers(0, 2, l.shape), l)
    c = np.where(rng.random(c.shape) < 0.72, (NA - 1) * rng.integers(0, 2, c.shape), c)
    f = np.where(rng.random(f.shape) < 0.7, (W0 - 1) * rng.integers(0, 2, f.shape), rng.integers(0, W0, f.shape))
    f[..., 0] = 0; f[..., W0 - 1] = W0 - 1
    l[:, 1::2, :, 0] = 0; l[:, 1::2, :, NA - 1] = W0 - 1
    c[:, :, 0, S - 1] = 0; c[:, :, 14, S - 1] = 0; c[:, :, 2, S - 1] = NA - 1; c[:, :, 15, S - 1] = NA - 1
    th = 4080 * rng.integers(0, 2, (N, 8, S))
    near = np.maximum(far(y, l, c, f) - rng.choice(np.array([0, 0, 1, 1, 1, 2, 9, 15, 16]), th.shape), 0)
    th = np.where(rng.random(th.shape) < 0.28, near, th)
    th[..., S - 1] = 0; th[:, 1::4, S - 1] = 4079
    th[np.arange(N), 2 * rng.integers(0, 4, N)] = 4080
    return pack(y, l, c, f, th)
def setup_inputs_corners(rng):
    y, l, c, f, th = parts(rng); x = np.arange(W0)
    th = np.where(rng.random(th.shape) < 0.25, 4080 * rng.integers(0, 2, th.shape), th)
    for r in range(N):
        o = rng.permutation(8)
        for g in range(8):
            f[r, g] = (x, np.maximum(x - 1, 0), (x + 1) % W0, x ^ 1, x * 0, x * 0 + W0 - 1, rng.choice(np.array([0, M - 1, M, W0 - 1]), W0), W0 - 1 - x)[int(o[g])]
            j = int(rng.integers(0, 6)); h = int(rng.integers(0, 6))
            if o[g] == 0: j = 5; h = 1; th[r, g] = 0
            if o[g] == 2: th[r, g] = 4080
            if j == 0: l[r, g] = np.arange(NA) % M
            if j == 1: l[r, g] = rng.choice(np.array([0, M - 1, M, W0 - 1]), (16, NA))
            if j == 2: l[r, g] = rng.integers(M, W0, (16, NA))
            if j == 3: l[r, g] = rng.integers(0, M, (16, NA))
            if j == 4: l[r, g, 1::2] = W0 - 1
            if h == 0: c[r, g] = c[r, g, :1]
            if h == 1: c[r, g] = np.arange(M) % NA
            if h == 2: c[r, g] = rng.choice(np.array([0, NA - 1]), (16, M))
            if h == 3: c[r, g] = (np.arange(M)[None, :] * 7 + np.arange(16)[:, None]) % NA
    return pack(y, l, c, f, th)
def setup_inputs_crowd(rng):
    y, l, c, f, th = parts(rng); y = rng.integers(0, 8, y.shape); th = rng.integers(25, 60, th.shape); i = np.arange(S)
    for r in range(N):
        for g in range(8):
            m = (1, 1, 2, 2, 16, 16, 1, 1)[g]; o = rng.permutation(NA); a = o[:m]
            x = int(rng.integers(M - S, M)) if g % 4 < 2 else int(rng.integers(M, W0))
            if r == N - 1 and g > 5: x = W0 - 1
            y[r, g, :, x] = 255; f[r, g, x] = x; l[r, g][:, a] = x
            c[r, g][rng.integers(0, 16, S), i] = a[i % m]
            if g in (1, 3, 4, 6):
                e = int(rng.integers(0, S)); f[r, g, e] = e; l[r, g, :, o[m]] = e; c[r, g, :, e] = o[m]
    return pack(y, l, c, f, th)
def setup_inputs_ties(rng):
    y, l, c, f, th = parts(rng)
    step = rng.choice(np.array([1, 3]), (1, 8, 1)); low = np.array([0, 127, 200, 252, 0, 127, 200, 252])[rng.permutation(8)].reshape(1, 8, 1)
    o = rng.permutation(8); step[0, o[:2]] = 1
    y = low[..., None] + step[..., None] * rng.integers(0, 2, y.shape)
    th = step * rng.integers(0, 11, th.shape)
    for g in o[:2]:
        y[:, g, 0] = low[0, g, 0]; th[:, g] = 0
        for r in range(N):
            e = int(rng.integers(0, S)); b = int(rng.integers(0, NA))
            f[r, g, e] = e; l[r, g, :, b] = e; c[r, g, :, e] = b
    B = NA // RO
    for r in range(N):
        for j in (2, 3):
            g = int(o[j]); e = int(rng.integers(0, S)); h = int(rng.integers(0, 16)); x = int(rng.integers(40, 175)); d = int(rng.integers(4, 41))
            s = np.array([x, x, x + d, x - d, x + 2 * d]) if j == 2 else np.array([x, x + 1, x + 1 + d, x + 1, x + 1 + d])
            y[r, g, :, :RO * S] = rng.integers(0, 256, (16, 1)); y[r, g, h, :RO * S] = np.repeat(s[:RO], S); y[r, g, h, (RO - 1) * S + e] = s[RO]
            f[r, g, :RO * S] = np.arange(RO * S)
            for t in range(RO):
                c[r, g, :, t * S:(t + 1) * S] = rng.integers(t * B, (t + 1) * B, (16, S))
                l[r, g, :, t * B:(t + 1) * B] = (t + 1) * S + (e + rng.integers(1, S, (16, B))) % S if t < RO - 1 else t * S + e
            if j == 2: th[r, g] = (1 + r % (RO - 1)) * d - 1
            else:
                k = 1 + r % 3; th[r, g] = d - rng.integers(1, k + 1, S); th[r, g, rng.permutation(S)[:k]] = 0
    w = far(y, l, c, f); th[:, o[4:6]] = w[:, o[4:6]]; g = int(o[5])
    for r in range(N): th[r, g, np.argsort(-w[r, g])[:1 + r % 3]] -= 1
    return pack(y, l, c, f, np.maximum(th, 0))
def check_inputs(d):
    bad = []
    for k, lo, hi in (("y0", 0, 255), ("lk", 0, W0 - 1), ("cl", 0, NA - 1), ("fw0", 0, W0 - 1), ("th", 0, 4080)):
        z = np.asarray(d[k]).astype(np.float64)
        if not np.all((z >= lo) & (z <= hi)): bad.append("range of " + k)
        elif not np.all(z == np.floor(z)): bad.append("whole numbers in " + k)
    return bad
def at(z, k):
    return np.take_along_axis(z, k[:, :, None, :], 2)[:, :, 0]
def reference(y0, lk, cl, fw0, th):
    Y = np.zeros((N, 8, 16, W), np.int64); Y[..., :W0] = y0.astype(np.float32).astype(np.int64).reshape(N, 8, 16, W0)
    L = lk.astype(np.int64).reshape(N, 8, 16, NA)
    C = np.zeros((N, 8, 16, W), np.int64); C[..., :M] = cl.astype(np.int64).reshape(N, 8, 16, M)
    F = np.tile(np.arange(W), (N, 8, 1)); F[:, :, :W0] = np.stack([gentries(z) for z in fw0])
    lane = np.arange(S); v = np.tile(lane, (N, 8, 1)); A = np.zeros((N, 8), np.int64); lim = th.astype(np.int64).reshape(N, 8, S)
    rk = np.arange(N)[:, None, None]; gr = np.arange(8)[None, :, None]; row = np.arange(16)[None, None, :, None]
    rk4 = rk[..., None]; gr4 = gr[..., None]
    for t in range(RO):
        a = np.take_along_axis(C, v[:, :, None, :], 3)
        b = np.take_along_axis(L, a, 3); c = L[rk4, gr4, (row + 5) % 16, a]
        fb = F[rk4, gr4, b].reshape(N, 8, 1, 16 * S); fc = F[rk4, gr4, c].reshape(N, 8, 1, 16 * S)
        y = ((np.take_along_axis(Y, fb, 3) + np.take_along_axis(Y, fc, 3)) >> 1).reshape(N, 8, 16, 16, S)
        own = np.take_along_axis(Y, v[:, :, None, :], 3)
        D = np.add.reduce(np.abs(y - own[:, :, :, None, :]), axis=2)
        p = np.argmax(D, axis=2); q = np.argmin(D, axis=2)
        big = at(D, p) > lim + (A % 16)[:, :, None]
        ap = at(a, p); bp = at(b, p); bq = at(b, q)
        yp = np.take_along_axis(y, p[:, :, None, None, :], 3)[:, :, :, 0]; yq = np.take_along_axis(y, q[:, :, None, None, :], 3)[:, :, :, 0]
        n = W0 + t * S + lane; new = own + np.sign(yq - own); u = np.add.reduce(own, axis=2)
        Y[..., W0 + t * S:W0 + (t + 1) * S] = yp
        C[..., W0 + t * S:W0 + (t + 1) * S] = a
        C[rk, gr, p, v] = (ap + u + t + 1) % NA
        Y[rk4, gr4, row, v[:, :, None, :]] = new
        for r in range(N):
            for s in range(N - 1): Y[r, :, :, M + s * S:M + (s + 1) * S] = new[(r + 1 + s) % N]
        for i in range(S - 1, -1, -1):
            i0, i1 = np.nonzero(big[:, :, i])
            L[i0, i1, 1::2, ap[i0, i1, i]] = n[i]
        F[rk, gr, v] = np.where(big, F[rk, gr, v], F[rk, gr, bq])
        F = np.take_along_axis(F, F, 2)
        w = F[rk, gr, bp]
        v = np.where((w < M) | (w >= W0), w - w % S + lane, np.where(big, n, (v + S) % M))
        A = np.add.reduce(big.astype(np.int64), axis=2)
    return {"yo": Y.reshape(N, 128, W).astype(np.float32).astype(BF), "lo": L.reshape(N, 128, NA).astype(np.float32), "fo": np.stack([gtable(z) for z in F]).astype(np.float32)}

@@ -1,0 +1,546 @@
+from concourse.bass import DstId, RemoteDMATransfer
+from concourse.mybir import AluOpType, AxisListType, ActivationFunctionType
+
+RO = 4
+BIG = 262144.0
+MAG = 402653184.0
+F32, BF, I32, U16, F16 = "float32", "bfloat16", "int32", "uint16", "float16"
+
+SCRATCH = {}
+
+
+def _s(name, cols, dtype, where="sbuf"):
+    SCRATCH[name] = (where, [128] + (cols if isinstance(cols, list) else [cols]), dtype)
+
+
+for _n, _c, _d in (
+        ("Y", 1408, BF), ("C", 1024, I32), ("LI", 1024, I32), ("L", 1152, F32), ("LT", 1024, BF), ("LO", 1152, F32),
+        ("FW", 56, I32), ("FL", 88, U16), ("FR0", 1536, F32), ("FR1", 1536, F32), ("W", 1408, BF), ("TH8", 128, I32),
+        ("THF", 128, F32), ("BT8", 128, F32), ("T4", 128, I32),
+        ("a16", 128, U16), ("af", 128, F32), ("Lg", 2048, F16), ("bc16", 256, U16), ("bt", 128, F32),
+        ("xb", 2048, F32), ("y16", 2048, F16), ("dS", 2048, BF), ("dA", [8, 256], BF),
+        ("own", 128, BF), ("nown", 128, F16), ("u1", 128, F32), ("SC", 256, F32), ("hi", 16, F32), ("pkc", 16, F32),
+        ("of", 16, F32), ("po", 16, U16), ("pr", [3, 128], F16), ("nrm", 128, F16), ("sg", 128, BF),
+        ("l16", 16, U16), ("er", 128, F32), ("em", 128, F32), ("es", 128, F32), ("e16", 8, U16), ("fx", 128, F32),
+        ("wm", 128, F32), ("ws", 128, F32), ("w16", 8, U16), ("wm2", 128, F32), ("ws2", 128, F32),
+        ("lamA", 8, F32), ("ap16", 8, U16), ("DD", 1024, BF), ("DS", 1024, BF), ("LE", 128, F32), ("ODDN", 128, F32),
+        ("um", 128, F32), ("cn", 128, I32), ("cm", 128, I32),
+        ("REF", 8, F32), ("NREF", 8, F32), ("thr", 8, F32), ("thr0", 8, F32), ("ar", 1, F32), ("arh", 1, F16), ("ai", 1, I32),
+        ("aj", 1, I32), ("ak", 1, F32),
+        ("vB", 8, F32), ("v16", 8, U16), ("vf", 8, F32), ("vo", 8, F32), ("vp", 8, F32), ("vo16", 8, U16),
+        ("t1", 8, F32), ("t2", 8, F32), ("t3", 8, F32), ("lo16", 8, U16),
+        ("al0", 8, F32), ("al1", 8, I32), ("al2", 8, I32), ("al3", 8, F32), ("al4", 8, F32), ("alt", 8, F32), ("aln", 8, F32),
+        ("wi", 8, I32), ("wB", 8, I32), ("gh", 8, F32), ("ng", 8, F32), ("x1", 8, F32), ("ga", 8, F32), ("gb", 8, F32),
+        ("FO", 88, F32), ("FOt", 88, F32),
+        ("T1", 128, I32), ("T1a", 128, I32), ("T2", 128, I32), ("T2a", 128, I32), ("M1", 2048, BF), ("I16", 128, F16),
+        ("If", 128, F32), ("BO", 128, F16), ("I5", 128, F16), ("E", 2048, F16), ("E5", 2048, F16), ("EF", 2048, F32),
+        ("OHf", 16, F32), ("Z32", 144, BF), ("Z1", 144, F16), ("zb", 512, BF), ("MK", 128, F32), ("MKH", 128, F32),
+        ("d0P", 128, F32), ("d0Q", 128, F32), ("d0S", 128, F32), ("d0D", 1024, BF), ("JR", 128, F32)):
+    _s(_n, _c, _d)
+for _n, _c, _d in (
+        ("SMI", 64, I32), ("SMF", 64, F32), ("CL", 8, U16),
+        ("NEW", 512, BF), ("LAND", 1536, BF)):
+    _s(_n, _c, _d)
+for _n in ("psb0", "psb1", "psd0", "psd1", "psd2", "psd3", "psk", "psm"):
+    _s(_n, 512, F32, "psum")
+
+SEMAPHORES = ["dv", "ac", "pe", "gp"] + ["in%d" % i for i in range(8)] + ["out%d" % i for i in range(8)] + \
+             ["arr%d" % t for t in range(RO)] + ["snt%d" % t for t in range(RO)]
+
+
+def rank_program(g, core, T, topo):
+    rank = T.rank_of(core)
+    if rank is None:
+        return
+    cores = T.cores
+    add, sub, mul, mx, mn = AluOpType.add, AluOpType.subtract, AluOpType.mult, AluOpType.max, AluOpType.min
+    ge, gt, le, lt, eq, ne = (AluOpType.is_ge, AluOpType.is_gt, AluOpType.is_le, AluOpType.is_lt, AluOpType.is_equal,
+                              AluOpType.not_equal)
+    AF = ActivationFunctionType
+    queues = {"v": g.vector, "a": g.scalar, "p": g.tensor, "g": g, "s": g.sync}
+    semof = {"v": "dv", "a": "ac", "p": "pe", "g": "gp"}
+    count = {"dv": 0, "ac": 0, "pe": 0, "gp": 0}
+    known = {"v": {}, "a": {}, "p": {}, "g": {}, "s": {}}
+    log = {}
+    total = {}
+
+    def waits(e, reads, writes):
+        need = {}
+        for toks, wr in ((reads, False), (writes, True)):
+            for nm, lo, hi in toks:
+                ps = nm[:2] == "ps"
+                for ent in log.get(nm, []):
+                    if ps:
+                        if ent[3] == e:
+                            continue
+                    elif ent[1] <= lo or ent[0] >= hi or not (wr or ent[2]):
+                        continue
+                    if ent[4] not in need or need[ent[4]][0] < ent[5]:
+                        need[ent[4]] = (ent[5], ent[6])
+        for sem in sorted(need, key=lambda s: -len(need[s][1])):
+            val, clk = need[sem]
+            k = known[e]
+            if k.get(sem, 0) >= val:
+                continue
+            queues[e].wait_ge(T.sem[sem], val)
+            k[sem] = val
+            for s2 in clk:
+                if k.get(s2, 0) < clk[s2]:
+                    k[s2] = clk[s2]
+
+    def note(e, reads, writes, sem, val):
+        clk = dict(known.get(e, {}))
+        for toks, wr in ((reads, False), (writes, True)):
+            for nm, lo, hi in toks:
+                ents = log.setdefault(nm, [])
+                if nm[:2] == "ps":
+                    ents[:] = []
+                elif wr:
+                    ents[:] = [x for x in ents if not (x[0] >= lo and x[1] <= hi)]
+                ents.append((lo, hi, wr, e, sem, val, clk))
+
+    def do(e, fn, reads, writes):
+        waits(e, reads, writes)
+        sem = semof[e]
+        count[sem] += 1
+        fn().then_inc(T.sem[sem], 1)
+        note(e, reads, writes, sem, count[sem])
+
+    def dma(e, out, in_, reads, writes, sem):
+        waits(e, reads, writes)
+        queues[e].dma_start(out=out, in_=in_).then_inc(T.sem[sem], 16)
+        total[sem] = 16
+        note("d" + sem, reads, writes, sem, 16)
+        log_clk = dict(known[e])
+        for nm, lo, hi in reads + writes:
+            for j in range(len(log[nm])):
+                if log[nm][j][4] == sem:
+                    log[nm][j] = log[nm][j][:6] + (log_clk,)
+
+    def A(nm, lo=0, hi=None, st=1):
+        if hi is None:
+            hi = SCRATCH[nm][1][1]
+        ap = T[nm][:, lo:hi] if st == 1 else T[nm][:, lo:hi:st]
+        return (ap, [(nm, lo, hi)], [])
+
+    def A8(nm):
+        return (T[nm][0:8, :], [(nm, 0, 128)], [])
+
+    def PR(q):
+        return (T.pr[:, q, :], [("pr", q, q + 1)], [])
+
+    def ind(win, off):
+        return (win[0].indirect(off[0]), win[1], off[1])
+
+    def vcopy(o, x):
+        do("v", lambda: g.vector.tensor_copy(out=o[0], in_=x[0]), x[1] + x[2] + o[2], o[1])
+
+    def vtt(o, x, y, op):
+        do("v", lambda: g.vector.tensor_tensor(out=o[0], in0=x[0], in1=y[0], op=op), x[1] + x[2] + y[1] + o[2], o[1])
+
+    def vts(o, x, s1, op0, s2=None, op1=None):
+        rd = x[1] + x[2] + o[2]
+        a1, a2 = s1, s2
+        if isinstance(s1, tuple):
+            rd = rd + s1[1]
+            a1 = s1[0]
+        if isinstance(s2, tuple):
+            rd = rd + s2[1]
+            a2 = s2[0]
+        if op1 is None:
+            do("v", lambda: g.vector.tensor_scalar(out=o[0], in0=x[0], scalar1=a1, scalar2=None, op0=op0), rd, o[1])
+        else:
+            do("v", lambda: g.vector.tensor_scalar(out=o[0], in0=x[0], scalar1=a1, scalar2=a2, op0=op0, op1=op1), rd, o[1])
+
+    def vscan(o, d0, d1, init, op0, op1):
+        do("v", lambda: g.vector.tensor_tensor_scan(out=o[0], data0=d0[0], data1=d1[0], initial=init, op0=op0, op1=op1),
+           d0[1] + d1[1], o[1])
+
+    def vset(o, c):
+        do("v", lambda: g.vector.memset(o[0], c), [], o[1])
+
+    def act(o, x, f, bias=None, scale=None):
+        rd = x[1] + x[2]
+        kw = {}
+        for key, z in (("bias", bias), ("scale", scale)):
+            if isinstance(z, tuple):
+                rd = rd + z[1]
+                kw[key] = z[0]
+            elif z is not None:
+                kw[key] = z
+        do("a", lambda: g.scalar.activation(out=o[0], in_=x[0], func=f, **kw), rd, o[1])
+
+    def mms(out_toks, reads, jobs):
+        def fn():
+            last = None
+            for o, l, r, st, sp in jobs:
+                last = g.tensor.matmul(out=o, lhsT=l, rhs=r, start=st, stop=sp)
+            return last
+        do("p", fn, reads, out_toks)
+
+    def iota(o, pattern, base, cmul, flag=False):
+        if flag:
+            do("g", lambda: g.iota(o[0], pattern=pattern, base=base, channel_multiplier=cmul,
+                                   allow_small_or_imprecise_dtypes=True), [], o[1])
+        else:
+            do("g", lambda: g.iota(o[0], pattern=pattern, base=base, channel_multiplier=cmul), [], o[1])
+
+    def SF(j, n=1):
+        return A("SMF", j, j + n)
+
+    RC, EV, OD, LIc, K15, TRc, TD = SF(0), SF(1), SF(2), SF(8, 8), SF(16, 8), SF(24, 8), SF(32, 8)
+
+    dma("s", T.C[:, 512:640], T.cl[:, 0:128], [], [("C", 512, 640)], "in0")
+    dma("a", T.FW[:, :], T.fw0[:, :], [], [("FW", 0, 56)], "in1")
+    dma("s", T.LI[:, :], T.lk[:, :], [], [("LI", 0, 1024)], "in2")
+    dma("a", T.Y[:, 512:1408], T.y0[:, :], [], [("Y", 512, 1408)], "in3")
+    dma("s", T.C[:, 640:1024], T.cl[:, 128:512], [], [("C", 640, 1024)], "in4")
+    dma("s", T.TH8[0:8, :], T.th[:, :], [], [("TH8", 0, 128)], "in5")
+
+    iota(A("T1"), [[1, 128]], 128, -1)
+    iota(A("T2"), [[16, 8], [0, 16]], 15, -1)
+    iota(A("SMI", 0, 1), [[0, 1]], 0, 1)
+    iota(A("SMI", 32, 64), [[16, 32]], 0, 0)
+    iota(A("FR1", 128, 1536), [[1, 1408]], 0, 0, True)
+    iota(A("JR"), [[1, 128]], 0, 0, True)
+    iota(A("SMI", 16, 24), [[1, 8]], 0, 0)
+    iota((T.T4[0:8, :], [("T4", 0, 128)], []), [[1, 128]], 0, -16)
+
+    vts(A("T1a"), A("T1"), 15, AluOpType.bitwise_and)
+    vts(A("T2a"), A("T2"), 4, AluOpType.arith_shift_right)
+    vts(A("I16"), A("T1"), 128, eq)
+    vts(A("M1", 0, 128), A("T1a"), 0, eq)
+    vts(A("BO"), A("T2a"), 0, eq)
+    vts(A("SMI", 1, 2), A("SMI", 0, 1), 15, AluOpType.bitwise_and)
+    vts(A("SMI", 2, 3), A("SMI", 0, 1), 1, AluOpType.bitwise_and)
+    vts(A("FL", 32, 88), A("FW"), 512, add)
+    vcopy(A("M1", 128, 256), A("M1", 0, 128))
+    vcopy(RC, A("SMI", 1, 2))
+    vts(A("FL", 0, 32), A("SMI", 32, 64), RC, add)
+    vset(A("Y", 0, 512), 0.0)
+    vset(A("W", 0, 512), 0.0)
+    for k in range(16):
+        vts(A("E", 128 * k, 128 * k + 128), A("I16"), A("M1", k, k + 1), mul)
+    vcopy(A("OHf"), A("M1", 0, 16))
+    vts(A("If"), A("T1"), 128, eq)
+    vtt(A("I5"), A("M1", 5, 133), A("BO"), mul)
+    vts(A("v16"), A("SMI", 32, 40), RC, add, 512, add)
+    vcopy(A("a16"), A("C", 512, 640))
+
+    act(A("W", 512, 1408), ind(A("Y"), A("FL", 32, 88)), AF.Copy, scale=0.5)
+    act(A("own"), ind(A("Y", 0, 1024), A("v16")), AF.Copy)
+    for j in (256, 512, 1024):
+        act(A("M1", j, 2 * j), A("M1", 0, j), AF.Copy)
+
+    FRc = "FR0"
+
+    def late_constants():
+        vset(A("zb"), 0.0)
+        vset(A("Z32"), 0.0)
+        vcopy(A("Z32", 16, 144, 16), A("BO", 0, 128, 16))
+        vcopy(A("Z1"), A("Z32"))
+        vts(A("Z32", 16, 144, 16), A("BO", 0, 128, 16), 32.0, mul)
+        vset(A("d0P"), 1.0)
+        vset(A("d0P", 0, 128, 16), -BIG)
+        vset(A("d0Q"), -1.0)
+        vset(A("d0Q", 0, 128, 16), BIG)
+        vts(LIc, A("SMI", 32, 40), RC, add)
+        vts(K15, LIc, 16.0, mul, 15.0, add)
+
+    def later_constants():
+        vcopy(A("MK"), A("M1", 0, 128))
+        vset(A("d0S"), 1.0)
+        vset(A("d0S", 0, 128, 16), 0.0)
+        vts((T.T4[0:8, :], [("T4", 0, 128)], []), (T.T4[0:8, :], [("T4", 0, 128)], []), 4, AluOpType.arith_shift_right)
+        vts(A8("BT8"), A8("T4"), 0, eq)
+        vcopy(A8("THF"), A8("TH8"))
+        mms([("psk", 0, 512)], [("BT8", 0, 128), ("THF", 0, 128)],
+            [(T.psk[:, 128:256], T.BT8[0:8, :], T.THF[0:8, :], True, True)])
+        vtt(A("em"), A("psk", 128, 256), A("MK"), mul)
+        vscan(A("es"), A("d0S"), A("em"), 0.0, mul, add)
+        vts(A("thr0"), A("es", 15, 128, 16), 32.0, mul, 15.0, add)
+        vcopy(A("thr"), A("thr0"))
+        vcopy(OD, A("SMI", 2, 3))
+        vts(EV, OD, -1.0, mul, 1.0, add)
+        vts(TRc, LIc, 1024.0, add)
+        vts(TD, LIc, 1.0 / 256, mul, -127.0 / 256, add)
+        vts(A("MKH"), A("MK"), 0.5, mul)
+        vset(A("d0D"), -1.0 / 256)
+        vset(A("d0D", 0, 1024, 128), 2048.0)
+        vcopy(A("CL"), A("SMI", 16, 24))
+        vset(A("C", 0, 512), 0)
+        vset(A("vB"), 512.0)
+        vcopy(A("L", 0, 1024), A("LI"))
+
+    def extract_f(FN, t):
+        jobs = []
+        lo = 640
+        for r in range(16):
+            jobs.append((T.psm[:, 0:56], T.EF[:, 128 * r:128 * r + 128], T[FN][:, lo + r:1536:16], r == 0, r == 15))
+        if t > 0:
+            for r in range(16):
+                jobs.append((T.psm[:, 64:64 + 8 * t], T.EF[:, 128 * r:128 * r + 128], T[FN][:, 128 + r:128 + 128 * t:16],
+                             r == 0, r == 15))
+        mms([("psm", 0, 512)], [("EF", 0, 2048), (FN, 128, 1536)], jobs)
+
+    for t in range(RO):
+        last = t == RO - 1
+        FRn = "FR1" if FRc == "FR0" else "FR0"
+        if t > 0:
+            vcopy(A("a16"), ind(A("C"), A("v16")))
+            act(A("own"), ind(A("Y", 0, 1024), A("v16")), AF.Copy)
+            vcopy(ind(A(FRc, 0, 1536), A("vo16")), A("fx"))
+            extract_f(FRc, t - 1)
+
+        def gather_links(h):
+            src = A("LI") if t == 0 else A("L", 0, 1024)
+            vcopy(A("Lg", 1024 * h, 1024 * h + 1024), ind(src, A("a16", 64 * h, 64 * h + 64)))
+
+        def lists(h):
+            jobs = []
+            for z, nm in ((0, "E"), (64, "E5")):
+                for k in range(16):
+                    jobs.append((T["psb%d" % h][:, z:z + 64], T[nm][:, 128 * k:128 * k + 128],
+                                 T.Lg[:, 1024 * h + k:1024 * h + 1024:16], k == 0, k == 15))
+            mms([("psb%d" % h, 0, 512)], [("E", 0, 2048), ("E5", 0, 2048), ("Lg", 1024 * h, 1024 * h + 1024)], jobs)
+
+        def lists_out(h):
+            vts(A("bc16", 128 * h, 128 * h + 128), A("psb%d" % h, 0, 128), 512.0, add)
+
+        def own_in(n):
+            ps = T["psd%d" % n]
+            jobs = [(ps[:, :], T.Z32[:, 0:128], T.zb[:, :], True, False)]
+            for k in range(16):
+                jobs.append((ps[:, k:512:16], T.I16[:, :], T.nown[:, 32 * n:32 * n + 32], False, False))
+            mms([("psd%d" % n, 0, 512)], [("Z32", 0, 144), ("zb", 0, 512), ("I16", 0, 128), ("nown", 0, 128)], jobs)
+
+        def blend_b(n):
+            o = 128 * (n // 2) + 32 * (n % 2)
+            act(A("xb", 512 * n, 512 * n + 512), ind(A("W"), A("bc16", o, o + 32)), AF.Copy, bias=1087.75)
+
+        def blend_c(n):
+            o = 128 * (n // 2) + 64 + 32 * (n % 2)
+            vtt(A("y16", 512 * n, 512 * n + 512), ind(A("W"), A("bc16", o, o + 32)), A("xb", 512 * n, 512 * n + 512), add)
+            mms([("psd%d" % n, 0, 512)], [("I16", 0, 128), ("y16", 512 * n, 512 * n + 512)],
+                [(T["psd%d" % n][:, :], T.I16[:, :], T.y16[:, 512 * n:512 * n + 512], False, True)])
+
+        def size_d(n):
+            for c in (0, 1):
+                act((T.dA[:, 2 * n + c, :], [("dA", 2 * n + c, 2 * n + c + 1)], []),
+                    A("psd%d" % n, 256 * c, 256 * c + 256), AF.Abs)
+
+        def keep_d(n):
+            vcopy(A("dS", 512 * n, 512 * n + 512), A("psd%d" % n))
+
+        def sum_d(h):
+            jobs = []
+            for r in range(16):
+                jobs.append((T.psk[:, 64 * h:64 * h + 64], T.Z32[:, 16 - r:144 - r],
+                             T.dA[:, 4 * h:4 * h + 4, 16 * r:16 * r + 16], r == 0, r == 15))
+            mms([("psk", 0, 512)], [("Z32", 0, 144), ("dA", 4 * h, 4 * h + 4)], jobs)
+
+        gather_links(0)
+        if t == 0:
+            for k in range(16):
+                z = (k + 5) % 16
+                vts(A("E5", 128 * k, 128 * k + 128), A("I5"), A("M1", z, z + 1), mul)
+        lists(0)
+        if t > 0:
+            vcopy(A("FL", 32, 88), A("psm", 0, 56))
+            if t > 1:
+                vcopy(A("FL", 0, 8 * (t - 1)), A("psm", 64, 64 + 8 * (t - 1)))
+        vts(A("nown"), A("own"), -1.0, mul, -1088.0, add)
+        gather_links(1)
+        if t > 0:
+            p = t - 1
+            for s in range(1):
+                act(A("Y", 1024, 1408), A("LAND", 384 * p, 384 * p + 384), AF.Copy)
+            act(A("W", 512, 1408), ind(A("Y"), A("FL", 32, 88)), AF.Copy, scale=0.5)
+            act(A("W", 0, 128 * t), ind(A("Y"), A("FL", 0, 8 * t)), AF.Copy, scale=0.5)
+        if t == 0:
+            late_constants()
+        own_in(0)
+        lists(1)
+        for n in (1, 2, 3):
+            own_in(n)
+        mms([("psm", 0, 512)], [("BO", 0, 128), ("nown", 0, 128)], [(T.psm[:, 256:384], T.BO[:, :], T.nown[:, :], True, True)])
+        lists_out(0)
+        blend_b(0)
+        blend_b(1)
+        blend_c(0)
+        lists_out(1)
+        blend_c(1)
+        size_d(0)
+        keep_d(0)
+        blend_b(2)
+        blend_c(2)
+        size_d(1)
+        keep_d(1)
+        sum_d(0)
+        blend_b(3)
+        blend_c(3)
+        size_d(2)
+        keep_d(2)
+        size_d(3)
+        sum_d(1)
+        keep_d(3)
+        act(A("u1"), A("psm", 256, 384), AF.Identity, scale=-1.0, bias=A("ak") if False else None) if False else None
+        vts(A("u1"), A("psm", 256, 384), -1.0, mul, float(t + 1 - 17408), add)
+        vcopy(A("bt", 0, 64), A("bc16", 0, 64))
+        vcopy(A("bt", 64, 128), A("bc16", 128, 192))
+        vcopy(A("af"), A("a16"))
+        if t == 0:
+            later_constants()
+            for k in range(16):
+                act(A("EF", 128 * k, 128 * k + 128), A("If"), AF.Copy, scale=A("OHf", k, k + 1))
+            act(A("FR0", 640, 1536), ind(A("FR1", 128, 1536), A("FL", 32, 88)), AF.Copy)
+            act(A("FR0", 128, 640), A("FR1", 128, 640), AF.Copy)
+        if last:
+            vts(A("LT"), A("L", 0, 1024), 0.0, lt, 1408.0, mul)
+            vtt(A("LO", 0, 1024), A("L", 0, 1024), A("LT"), add)
+        LN = "LO" if last else "L"
+        vts(A("ODDN"), A("JR"), float(128 * t - 512 + (1408 if last else 0)), add, OD, mul)
+
+        vscan(A("SC", 0, 128), A("d0P"), A("psk", 0, 128), 0.0, add, mx)
+        vscan(A("SC", 128, 256), A("d0Q"), A("psk", 0, 128), 0.0, add, mn)
+        vts(A("hi"), A("SC", 15, 256, 16), MAG, add, MAG, sub)
+        vtt(A("pkc", 0, 8), K15, A("SC", 15, 128, 16), sub)
+        vtt(A("pkc", 8, 16), K15, A("SC", 143, 256, 16), add)
+        vtt(A("of", 0, 8), A("pkc", 0, 8), A("hi", 0, 8), add)
+        vtt(A("of", 8, 16), A("pkc", 8, 16), A("hi", 8, 16), sub)
+        vtt(A("NREF"), A("SC", 15, 128, 16), A("thr"), le)
+        vcopy(A("po"), A("of"))
+        vtt(A("REF"), A("SC", 15, 128, 16), A("thr"), gt)
+        P, Q = A("po", 0, 8), A("po", 8, 16)
+        act(A("sg"), ind(A("dS"), Q), AF.Sign)
+        vtt(PR(0), ind(A("M1"), Q), A("bt"), mul)
+        vtt(PR(1), ind(A("M1"), P), A("bt"), mul)
+        mms([("psb0", 0, 512)], [("Z1", 0, 144), ("pr", 0, 2)],
+            [(T.psb0[:, 0:16], T.Z1[:, 16 - r:144 - r], T.pr[:, 0:2, r:128:16], r == 0, r == 15) for r in range(16)])
+        vts(A("vp"), A("vB"), 128.0, add)
+        vtt(PR(2), ind(A("M1"), P), A("af"), mul)
+        vtt(A("nrm"), ind(A("NREF"), A("CL")), A("MKH"), mul)
+        mms([("psk", 0, 512)], [("Z1", 0, 144), ("pr", 2, 3)],
+            [(T.psk[:, 256:264], T.Z1[:, 16 - r:144 - r], T.pr[:, 2, r:128:16], r == 0, r == 15) for r in range(16)])
+        for nm in ("psb1", "psd0"):
+            mms([(nm, 0, 512)], [("BO", 0, 128), ("pr", 2, 3), ("nrm", 0, 128)],
+                [(T[nm][:, 0:128], T.BO[:, :], T.pr[:, 2, :], True, False), (T[nm][:, 0:128], T.BO[:, :], T.nrm[:, :], False, True)])
+        nw = A("NEW", 128 * t, 128 * t + 128)
+        vtt(nw, A("own"), A("sg"), add)
+        waits("g", nw[1], [])
+        used, transfers = set(), []
+        others = sorted([c for c in cores if c != core], key=lambda c: len(topo.engines(core, c)))
+        for c in others:
+            fewest = topo.engines(core, others[0])
+            eng = [e for e in topo.engines(core, c) if e not in used]
+            if len(topo.engines(core, c)) > len(fewest):
+                eng = [e for e in eng if e not in fewest]
+            eng = eng[:4]
+            used.update(eng)
+            s = (rank - T.rank_of(c) - 1) % len(cores)
+            rid, pid = topo.addr(c, core)
+            transfers.append(RemoteDMATransfer(dst_ids=[DstId(rid=rid, pnc=pid)], dma_engine_mask=sum(1 << e for e in eng),
+                                               remote_sem=T.sem["arr%d" % t], src=nw[0],
+                                               dst=T.LAND[:, 384 * t + 128 * s:384 * t + 128 * s + 128]))
+        g.remote_dma_fused(transfers, local_sem=T.sem["snt%d" % t])
+        total["arr%d" % t] = 12
+        total["snt%d" % t] = 12
+        note("r", [], [("LAND", 384 * t, 384 * t + 384)], "arr%d" % t, 12)
+
+        vtt(A("vo"), A("vp"), A("NREF"), mul)
+        vtt(A("vo"), A("vo"), LIc, add)
+        vcopy(A("l16"), A("psb0", 0, 16))
+        vcopy(A("vo16"), A("vo"))
+        vcopy(A("er"), ind(A(FRc, 128, 1536), A("l16", 0, 8)))
+        vcopy(A("lamA"), A("psk", 256, 264))
+        vcopy(A("ap16"), A("psk", 256, 264))
+        vcopy(ind(A(FRc, 0, 1536), A("vo16")), A("er"))
+        for c in range(4):
+            act(A("DD", 128 * c, 128 * c + 128), A("psd0", 0, 128), AF.Abs if False else AF.Identity, scale=-1.0,
+                bias=A("lamA", c, c + 1)) if False else None
+        for c in range(4):
+            act(A("DD", 128 * c, 128 * c + 128), A("psd0", 0, 128), AF.Abs, scale=-1.0, bias=A("lamA", c, c + 1))
+        act(A("LE"), ind(A(LN, 0, 1024), A("ap16")), AF.Copy, scale=EV)
+        act(A(FRn, 640, 1536), ind(A(FRc, 128, 1536), A("FL", 32, 88)), AF.Copy)
+        if t > 0:
+            act(A(FRn, 128, 128 + 128 * t), ind(A(FRc, 128, 1536), A("FL", 0, 8 * t)), AF.Copy)
+        if not last:
+            vtt(A("wm"), ind(A(FRc, 128, 1536), A("l16", 8, 16)), A("MK"), mul)
+            vtt(A("em"), A("er"), A("MK"), mul)
+            vscan(A("ws"), A("d0S"), A("wm"), 0.0, mul, add)
+            vscan(A("es"), A("d0S"), A("em"), 0.0, mul, add)
+            vcopy(A("w16"), A("ws", 15, 128, 16))
+            vcopy(A("e16"), A("es", 15, 128, 16))
+            vtt(A("wm2"), ind(A(FRc, 128, 1536), A("w16")), A("MK"), mul)
+            vts(A("al0"), A("vB"), 512.0, ge, 128.0, mul)
+            vscan(A("ws2"), A("d0S"), A("wm2"), 0.0, mul, add)
+            vtt(A("al1"), A("vB"), A("al0"), add)
+        else:
+            vtt(A("em"), A("er"), A("MK"), mul)
+            vscan(A("es"), A("d0S"), A("em"), 0.0, mul, add)
+            vcopy(A("e16"), A("es", 15, 128, 16))
+        vcopy(A("fx"), ind(A(FRc, 128, 1536), A("e16")))
+        for c in range(4, 8):
+            vts(A("DD", 128 * c, 128 * c + 128), A("psb1", 0, 128), A("lamA", c, c + 1), ne)
+        vtt(A("t1"), A("lamA"), TRc, sub)
+        vscan(A("DS"), A("d0D"), A("DD"), 0.0, add, mn)
+        vtt(A("t1"), A("t1"), A("REF"), mul)
+        vtt(A("t2"), A("DS", 127, 1024, 128), TD, ge)
+        vtt(A("t3"), A("t2"), A("t1"), mul)
+        if not last:
+            vts(A("al2"), A("al1"), 384, AluOpType.bitwise_and)
+        vtt(A("t3"), A("t3"), TRc, add)
+        if not last:
+            vts(A("al3"), A("al2"), 512.0, add)
+        vcopy(A("lo16"), A("t3"))
+        if not last:
+            vtt(A("alt"), A("al3"), A("NREF"), mul)
+            vts(A("al4"), A("REF"), float(128 * t), mul)
+            vcopy(A("wi"), A("ws2", 15, 128, 16))
+            vtt(A("aln"), A("alt"), A("al4"), add)
+            vts(A("gh"), A("ws2", 15, 128, 16), 1024.0, ge)
+            vts(A("wB"), A("wi"), 1920, AluOpType.bitwise_and)
+            vts(A("ng"), A("ws2", 15, 128, 16), 1024.0, lt)
+            vtt(A("ga"), A("gh"), A("aln"), mul)
+            vtt(A("x1"), A("wB"), A("ng"), mul)
+            vtt(A("gb"), A("ga"), LIc, add)
+            vtt(A("vB"), A("x1"), A("ga"), add)
+            vtt(A("vf"), A("x1"), A("gb"), add)
+        vtt((ind(A(LN, 0, 1152), A("lo16"))), A("LE"), A("ODDN"), add)
+        vtt(A("Y", 128 * t, 128 * t + 128), ind(A("dS"), P), A("own"), add)
+        vcopy(ind(A("Y", 0, 1024), A("v16")), nw)
+        if not last:
+            vtt(A("um"), ind(A("M1"), P), A("u1"), mul)
+            vcopy(A("C", 128 * t, 128 * t + 128), A("a16"))
+            vtt(A("cn"), A("um"), A("af"), add)
+            vts(A("cm"), A("cn"), 1023, AluOpType.bitwise_and)
+            vcopy(ind(A("C"), A("v16")), A("cm"))
+            do("v", lambda: g.vector.tensor_reduce(out=T.ar[:, :], in_=T.REF[:, :], axis=AxisListType.X, op=add),
+               [("REF", 0, 8)], [("ar", 0, 1)])
+            vcopy(A("arh"), A("ar"))
+            mms([("psb0", 0, 512)], [("BO", 0, 128), ("arh", 0, 1)], [(T.psb0[:, 64:65], T.BO[:, :], T.arh[:, :], True, True)])
+            vcopy(A("v16"), A("vf"))
+            vcopy(A("ai"), A("psb0", 64, 65))
+            vts(A("aj"), A("ai"), 15, AluOpType.bitwise_and)
+            vts(A("ak"), A("aj"), 32.0, mul)
+            vts(A("thr"), A("thr0"), A("ak"), add)
+        FRc = FRn
+
+    dma("s", T.yo[:, 0:512], T.Y[:, 512:1024], [("Y", 512, 1024)], [], "out0")
+    dma("s", T.yo[:, 896:1408], T.Y[:, 0:512], [("Y", 0, 512)], [], "out1")
+    dma("s", T.lo[:, :], T.LO[:, 0:1024], [("LO", 0, 1024)], [], "out2")
+    vcopy(ind(A(FRc, 0, 1536), A("vo16")), A("fx"))
+    extract_f(FRc, RO - 1)
+    vts(A("FO", 80, 88), LIc, 1280.0, add)
+    vts(A("FOt", 0, 56), A("psm", 0, 56), 512.0, lt, 1408.0, mul)
+    vts(A("FOt", 56, 80), A("psm", 64, 88), 512.0, lt, 1408.0, mul)
+    vtt(A("FOt", 0, 56), A("psm", 0, 56), A("FOt", 0, 56), add)
+    vtt(A("FOt", 56, 80), A("psm", 64, 88), A("FOt", 56, 80), add)
+    vts(A("FO", 0, 80), A("FOt", 0, 80), -512.0, add)
+    dma("a", T.fo[:, :], T.FO[:, :], [("FO", 0, 88)], [], "out3")
+    p = 384 * (RO - 1)
+    dma("s", T.yo[:, 512:896], T.LAND[:, p:p + 384], [("LAND", p, p + 384)], [], "out4")
+    for sem in ("dv", "ac", "pe", "gp"):
+        g.wait_ge(T.sem[sem], count[sem])
+    for sem in sorted(total):
+        g.wait_ge(T.sem[sem], total[sem])

@@ -7,44 +7,34 @@ MAG = 402653184.0
 F32, BF, I32, U16, F16 = "float32", "bfloat16", "int32", "uint16", "float16"
 
 SCRATCH = {}
-
-
-def _s(name, cols, dtype, where="sbuf"):
-    SCRATCH[name] = (where, [128] + (cols if isinstance(cols, list) else [cols]), dtype)
-
-
 for _n, _c, _d in (
-        ("Y", 1408, BF), ("C", 1024, I32), ("LI", 1024, I32), ("L", 1152, F32), ("LT", 1024, BF), ("LO", 1152, F32),
+        ("Y", 1408, BF), ("C", 1024, I32), ("LI", 1024, I32), ("L", 1152, F32), ("LO", 1152, F32),
         ("FW", 56, I32), ("FL", 88, U16), ("FR0", 1536, F32), ("FR1", 1536, F32), ("W", 1408, BF), ("TH8", 128, I32),
-        ("THF", 128, F32), ("BT8", 128, F32), ("T4", 128, I32),
+        ("THF", 128, F32), ("BT8", 128, F32), ("T4", 128, I32), ("NEW", 512, BF), ("LAND", 1536, BF),
         ("a16", 128, U16), ("af", 128, F32), ("Lg", 2048, F16), ("bc16", 256, U16), ("bt", 128, F32),
         ("xb", 2048, F32), ("y16", 2048, F16), ("dS", 2048, BF), ("dA", [8, 256], BF),
         ("own", 128, BF), ("nown", 128, F16), ("u1", 128, F32), ("SC", 256, F32), ("hi", 16, F32), ("pkc", 16, F32),
         ("of", 16, F32), ("po", 16, U16), ("pr", [3, 128], F16), ("nrm", 128, F16), ("sg", 128, BF),
         ("l16", 16, U16), ("er", 128, F32), ("em", 128, F32), ("es", 128, F32), ("e16", 8, U16), ("fx", 128, F32),
-        ("wm", 128, F32), ("ws", 128, F32), ("w16", 8, U16), ("wm2", 128, F32), ("ws2", 128, F32),
+        ("wm", 128, F32), ("ws", 128, F32), ("w16", 8, U16),
         ("lamA", 8, F32), ("ap16", 8, U16), ("DD", 1024, BF), ("DS", 1024, BF), ("LE", 128, F32), ("ODDN", 128, F32),
-        ("um", 128, F32), ("cn", 128, I32), ("cm", 128, I32),
+        ("ODDO", 128, F32), ("um", 128, F32), ("cn", 128, I32), ("cm", 128, I32),
         ("REF", 8, F32), ("NREF", 8, F32), ("thr", 8, F32), ("thr0", 8, F32), ("ar", 1, F32), ("arh", 1, F16), ("ai", 1, I32),
-        ("aj", 1, I32), ("ak", 1, F32),
-        ("vB", 8, F32), ("v16", 8, U16), ("vf", 8, F32), ("vo", 8, F32), ("vp", 8, F32), ("vo16", 8, U16),
-        ("t1", 8, F32), ("t2", 8, F32), ("t3", 8, F32), ("lo16", 8, U16),
-        ("al0", 8, F32), ("al1", 8, I32), ("al2", 8, I32), ("al3", 8, F32), ("al4", 8, F32), ("alt", 8, F32), ("aln", 8, F32),
-        ("wi", 8, I32), ("wB", 8, I32), ("gh", 8, F32), ("ng", 8, F32), ("x1", 8, F32), ("ga", 8, F32), ("gb", 8, F32),
-        ("FO", 88, F32), ("FOt", 88, F32),
+        ("aj", 1, I32), ("ak", 1, F32), ("vB", 8, F32), ("v16", 8, U16), ("vf", 8, F32), ("vo", 8, F32), ("vq", 8, F32),
+        ("vp", 8, F32), ("vo16", 8, U16), ("t0", 8, F32), ("t1", 8, F32), ("t2", 8, F32), ("t3", 8, F32), ("t4", 8, F32),
+        ("lo16", 8, U16), ("al0", 8, F32), ("al1", 8, I32), ("al2", 8, I32), ("al3", 8, F32), ("al4", 8, F32), ("alt", 8, F32),
+        ("aln", 8, F32), ("wi", 8, I32), ("wB", 8, I32), ("gh", 8, F32), ("ng", 8, F32), ("x1", 8, F32), ("ga", 8, F32),
+        ("gb", 8, F32), ("FO", 88, F32), ("FOt", 88, F32), ("FOu", 88, F32),
         ("T1", 128, I32), ("T1a", 128, I32), ("T2", 128, I32), ("T2a", 128, I32), ("M1", 2048, BF), ("I16", 128, F16),
         ("If", 128, F32), ("BO", 128, F16), ("I5", 128, F16), ("E", 2048, F16), ("E5", 2048, F16), ("EF", 2048, F32),
         ("OHf", 16, F32), ("Z32", 144, BF), ("Z1", 144, F16), ("zb", 512, BF), ("MK", 128, F32), ("MKH", 128, F32),
-        ("d0P", 128, F32), ("d0Q", 128, F32), ("d0S", 128, F32), ("d0D", 1024, BF), ("JR", 128, F32)):
-    _s(_n, _c, _d)
-for _n, _c, _d in (
-        ("SMI", 64, I32), ("SMF", 64, F32), ("CL", 8, U16),
-        ("NEW", 512, BF), ("LAND", 1536, BF)):
-    _s(_n, _c, _d)
+        ("d0P", 128, F32), ("d0Q", 128, F32), ("d0S", 128, F32), ("d0D", 1024, BF), ("JR", 128, F32),
+        ("SMI", 64, I32), ("SMF", 64, F32), ("CL", 8, U16)):
+    SCRATCH[_n] = ("sbuf", [128] + (_c if isinstance(_c, list) else [_c]), _d)
 for _n in ("psb0", "psb1", "psd0", "psd1", "psd2", "psd3", "psk", "psm"):
-    _s(_n, 512, F32, "psum")
+    SCRATCH[_n] = ("psum", [128, 512], F32)
 
-SEMAPHORES = ["dv", "ac", "pe", "gp"] + ["in%d" % i for i in range(8)] + ["out%d" % i for i in range(8)] + \
+SEMAPHORES = ["dv", "ac", "pe", "gp"] + ["in%d" % i for i in range(6)] + ["out%d" % i for i in range(5)] + \
              ["arr%d" % t for t in range(RO)] + ["snt%d" % t for t in range(RO)]
 
 
@@ -56,6 +46,7 @@ def rank_program(g, core, T, topo):
     add, sub, mul, mx, mn = AluOpType.add, AluOpType.subtract, AluOpType.mult, AluOpType.max, AluOpType.min
     ge, gt, le, lt, eq, ne = (AluOpType.is_ge, AluOpType.is_gt, AluOpType.is_le, AluOpType.is_lt, AluOpType.is_equal,
                               AluOpType.not_equal)
+    band, shr = AluOpType.bitwise_and, AluOpType.arith_shift_right
     AF = ActivationFunctionType
     queues = {"v": g.vector, "a": g.scalar, "p": g.tensor, "g": g, "s": g.sync}
     semof = {"v": "dv", "a": "ac", "p": "pe", "g": "gp"}
@@ -88,8 +79,7 @@ def rank_program(g, core, T, topo):
                 if k.get(s2, 0) < clk[s2]:
                     k[s2] = clk[s2]
 
-    def note(e, reads, writes, sem, val):
-        clk = dict(known.get(e, {}))
+    def note(e, clk, reads, writes, sem, val):
         for toks, wr in ((reads, False), (writes, True)):
             for nm, lo, hi in toks:
                 ents = log.setdefault(nm, [])
@@ -104,18 +94,13 @@ def rank_program(g, core, T, topo):
         sem = semof[e]
         count[sem] += 1
         fn().then_inc(T.sem[sem], 1)
-        note(e, reads, writes, sem, count[sem])
+        note(e, dict(known[e]), reads, writes, sem, count[sem])
 
     def dma(e, out, in_, reads, writes, sem):
         waits(e, reads, writes)
         queues[e].dma_start(out=out, in_=in_).then_inc(T.sem[sem], 16)
         total[sem] = 16
-        note("d" + sem, reads, writes, sem, 16)
-        log_clk = dict(known[e])
-        for nm, lo, hi in reads + writes:
-            for j in range(len(log[nm])):
-                if log[nm][j][4] == sem:
-                    log[nm][j] = log[nm][j][:6] + (log_clk,)
+        note("d", dict(known[e]), reads, writes, sem, 16)
 
     def A(nm, lo=0, hi=None, st=1):
         if hi is None:
@@ -152,8 +137,8 @@ def rank_program(g, core, T, topo):
         else:
             do("v", lambda: g.vector.tensor_scalar(out=o[0], in0=x[0], scalar1=a1, scalar2=a2, op0=op0, op1=op1), rd, o[1])
 
-    def vscan(o, d0, d1, init, op0, op1):
-        do("v", lambda: g.vector.tensor_tensor_scan(out=o[0], data0=d0[0], data1=d1[0], initial=init, op0=op0, op1=op1),
+    def vscan(o, d0, d1, op0, op1):
+        do("v", lambda: g.vector.tensor_tensor_scan(out=o[0], data0=d0[0], data1=d1[0], initial=0.0, op0=op0, op1=op1),
            d0[1] + d1[1], o[1])
 
     def vset(o, c):
@@ -170,13 +155,13 @@ def rank_program(g, core, T, topo):
                 kw[key] = z
         do("a", lambda: g.scalar.activation(out=o[0], in_=x[0], func=f, **kw), rd, o[1])
 
-    def mms(out_toks, reads, jobs):
+    def mms(bank, reads, jobs):
         def fn():
             last = None
             for o, l, r, st, sp in jobs:
                 last = g.tensor.matmul(out=o, lhsT=l, rhs=r, start=st, stop=sp)
             return last
-        do("p", fn, reads, out_toks)
+        do("p", fn, reads, [(bank, 0, 512)])
 
     def iota(o, pattern, base, cmul, flag=False):
         if flag:
@@ -185,40 +170,50 @@ def rank_program(g, core, T, topo):
         else:
             do("g", lambda: g.iota(o[0], pattern=pattern, base=base, channel_multiplier=cmul), [], o[1])
 
+    def fill(o, c, flag=True):
+        iota(o, [[0, o[1][0][2] - o[1][0][1]]], c, 0, flag)
+
     def SF(j, n=1):
         return A("SMF", j, j + n)
 
     RC, EV, OD, LIc, K15, TRc, TD = SF(0), SF(1), SF(2), SF(8, 8), SF(16, 8), SF(24, 8), SF(32, 8)
 
-    dma("s", T.C[:, 512:640], T.cl[:, 0:128], [], [("C", 512, 640)], "in0")
-    dma("a", T.FW[:, :], T.fw0[:, :], [], [("FW", 0, 56)], "in1")
-    dma("s", T.LI[:, :], T.lk[:, :], [], [("LI", 0, 1024)], "in2")
-    dma("a", T.Y[:, 512:1408], T.y0[:, :], [], [("Y", 512, 1408)], "in3")
+    dma("s", T.LI[:, :], T.lk[:, :], [], [("LI", 0, 1024)], "in0")
+    dma("a", T.C[:, 512:640], T.cl[:, 0:128], [], [("C", 512, 640)], "in1")
+    dma("a", T.FW[:, :], T.fw0[:, :], [], [("FW", 0, 56)], "in2")
+    dma("s", T.Y[:, 512:1408], T.y0[:, :], [], [("Y", 512, 1408)], "in3")
     dma("s", T.C[:, 640:1024], T.cl[:, 128:512], [], [("C", 640, 1024)], "in4")
     dma("s", T.TH8[0:8, :], T.th[:, :], [], [("TH8", 0, 128)], "in5")
 
     iota(A("T1"), [[1, 128]], 128, -1)
-    iota(A("T2"), [[16, 8], [0, 16]], 15, -1)
     iota(A("SMI", 0, 1), [[0, 1]], 0, 1)
+    iota(A("T2"), [[16, 8], [0, 16]], 15, -1)
     iota(A("SMI", 32, 64), [[16, 32]], 0, 0)
-    iota(A("FR1", 128, 1536), [[1, 1408]], 0, 0, True)
-    iota(A("JR"), [[1, 128]], 0, 0, True)
     iota(A("SMI", 16, 24), [[1, 8]], 0, 0)
-    iota((T.T4[0:8, :], [("T4", 0, 128)], []), [[1, 128]], 0, -16)
+    iota(A8("T4"), [[1, 128]], 0, -16)
+    fill(A("Y", 0, 512), 0)
+    fill(A("W", 0, 512), 0)
+    fill(A("Z32"), 0)
+    fill(A("zb"), 0)
+    fill(A("d0P"), 1)
+    fill(A("d0Q"), -1)
+    fill(A("d0S"), 1)
+    fill(A("vB"), 512)
+    iota(A("JR"), [[1, 128]], 0, 0, True)
+    fill(A("C", 0, 512), 0, False)
+    iota(A("FR1", 128, 1536), [[1, 1408]], 0, 0, True)
 
-    vts(A("T1a"), A("T1"), 15, AluOpType.bitwise_and)
-    vts(A("T2a"), A("T2"), 4, AluOpType.arith_shift_right)
+    vts(A("T1a"), A("T1"), 15, band)
+    vts(A("T2a"), A("T2"), 4, shr)
     vts(A("I16"), A("T1"), 128, eq)
     vts(A("M1", 0, 128), A("T1a"), 0, eq)
     vts(A("BO"), A("T2a"), 0, eq)
-    vts(A("SMI", 1, 2), A("SMI", 0, 1), 15, AluOpType.bitwise_and)
-    vts(A("SMI", 2, 3), A("SMI", 0, 1), 1, AluOpType.bitwise_and)
+    vts(A("SMI", 1, 2), A("SMI", 0, 1), 15, band)
+    vts(A("SMI", 2, 3), A("SMI", 0, 1), 1, band)
     vts(A("FL", 32, 88), A("FW"), 512, add)
     vcopy(A("M1", 128, 256), A("M1", 0, 128))
     vcopy(RC, A("SMI", 1, 2))
     vts(A("FL", 0, 32), A("SMI", 32, 64), RC, add)
-    vset(A("Y", 0, 512), 0.0)
-    vset(A("W", 0, 512), 0.0)
     for k in range(16):
         vts(A("E", 128 * k, 128 * k + 128), A("I16"), A("M1", k, k + 1), mul)
     vcopy(A("OHf"), A("M1", 0, 16))
@@ -226,38 +221,35 @@ def rank_program(g, core, T, topo):
     vtt(A("I5"), A("M1", 5, 133), A("BO"), mul)
     vts(A("v16"), A("SMI", 32, 40), RC, add, 512, add)
     vcopy(A("a16"), A("C", 512, 640))
+    for k in range(16):
+        z = (k + 5) % 16
+        vts(A("E5", 128 * k, 128 * k + 128), A("I5"), A("M1", z, z + 1), mul)
 
     act(A("W", 512, 1408), ind(A("Y"), A("FL", 32, 88)), AF.Copy, scale=0.5)
     act(A("own"), ind(A("Y", 0, 1024), A("v16")), AF.Copy)
+    for k in range(16):
+        act(A("EF", 128 * k, 128 * k + 128), A("If"), AF.Copy, scale=A("OHf", k, k + 1))
     for j in (256, 512, 1024):
         act(A("M1", j, 2 * j), A("M1", 0, j), AF.Copy)
 
-    FRc = "FR0"
-
     def late_constants():
-        vset(A("zb"), 0.0)
-        vset(A("Z32"), 0.0)
         vcopy(A("Z32", 16, 144, 16), A("BO", 0, 128, 16))
         vcopy(A("Z1"), A("Z32"))
         vts(A("Z32", 16, 144, 16), A("BO", 0, 128, 16), 32.0, mul)
-        vset(A("d0P"), 1.0)
         vset(A("d0P", 0, 128, 16), -BIG)
-        vset(A("d0Q"), -1.0)
         vset(A("d0Q", 0, 128, 16), BIG)
         vts(LIc, A("SMI", 32, 40), RC, add)
         vts(K15, LIc, 16.0, mul, 15.0, add)
 
     def later_constants():
         vcopy(A("MK"), A("M1", 0, 128))
-        vset(A("d0S"), 1.0)
         vset(A("d0S", 0, 128, 16), 0.0)
-        vts((T.T4[0:8, :], [("T4", 0, 128)], []), (T.T4[0:8, :], [("T4", 0, 128)], []), 4, AluOpType.arith_shift_right)
+        vts(A8("T4"), A8("T4"), 4, shr)
         vts(A8("BT8"), A8("T4"), 0, eq)
         vcopy(A8("THF"), A8("TH8"))
-        mms([("psk", 0, 512)], [("BT8", 0, 128), ("THF", 0, 128)],
-            [(T.psk[:, 128:256], T.BT8[0:8, :], T.THF[0:8, :], True, True)])
+        mms("psk", [("BT8", 0, 128), ("THF", 0, 128)], [(T.psk[:, 128:256], T.BT8[0:8, :], T.THF[0:8, :], True, True)])
         vtt(A("em"), A("psk", 128, 256), A("MK"), mul)
-        vscan(A("es"), A("d0S"), A("em"), 0.0, mul, add)
+        vscan(A("es"), A("d0S"), A("em"), mul, add)
         vts(A("thr0"), A("es", 15, 128, 16), 32.0, mul, 15.0, add)
         vcopy(A("thr"), A("thr0"))
         vcopy(OD, A("SMI", 2, 3))
@@ -268,51 +260,38 @@ def rank_program(g, core, T, topo):
         vset(A("d0D"), -1.0 / 256)
         vset(A("d0D", 0, 1024, 128), 2048.0)
         vcopy(A("CL"), A("SMI", 16, 24))
-        vset(A("C", 0, 512), 0)
-        vset(A("vB"), 512.0)
-        vcopy(A("L", 0, 1024), A("LI"))
 
-    def extract_f(FN, t):
-        jobs = []
-        lo = 640
-        for r in range(16):
-            jobs.append((T.psm[:, 0:56], T.EF[:, 128 * r:128 * r + 128], T[FN][:, lo + r:1536:16], r == 0, r == 15))
-        if t > 0:
-            for r in range(16):
-                jobs.append((T.psm[:, 64:64 + 8 * t], T.EF[:, 128 * r:128 * r + 128], T[FN][:, 128 + r:128 + 128 * t:16],
-                             r == 0, r == 15))
-        mms([("psm", 0, 512)], [("EF", 0, 2048), (FN, 128, 1536)], jobs)
+    def to_list(bank, o, src, q):
+        return [(T[bank][:, o:o + 8 * q], T.Z1[:, 16 - r:144 - r], src(r), r == 0, r == 15) for r in range(16)]
 
+    FRc, FRn = "FR0", "FR1"
     for t in range(RO):
         last = t == RO - 1
-        FRn = "FR1" if FRc == "FR0" else "FR0"
-        if t > 0:
-            vcopy(A("a16"), ind(A("C"), A("v16")))
-            act(A("own"), ind(A("Y", 0, 1024), A("v16")), AF.Copy)
-            vcopy(ind(A(FRc, 0, 1536), A("vo16")), A("fx"))
-            extract_f(FRc, t - 1)
 
-        def gather_links(h):
+        def gather_links(q):
             src = A("LI") if t == 0 else A("L", 0, 1024)
-            vcopy(A("Lg", 1024 * h, 1024 * h + 1024), ind(src, A("a16", 64 * h, 64 * h + 64)))
+            vcopy(A("Lg", 512 * q, 512 * q + 512), ind(src, A("a16", 32 * q, 32 * q + 32)))
+
+        def list_at(h, z):
+            return ("psm", 400) if h and z else ("psb%d" % h, z)
 
         def lists(h):
-            jobs = []
             for z, nm in ((0, "E"), (64, "E5")):
-                for k in range(16):
-                    jobs.append((T["psb%d" % h][:, z:z + 64], T[nm][:, 128 * k:128 * k + 128],
-                                 T.Lg[:, 1024 * h + k:1024 * h + 1024:16], k == 0, k == 15))
-            mms([("psb%d" % h, 0, 512)], [("E", 0, 2048), ("E5", 0, 2048), ("Lg", 1024 * h, 1024 * h + 1024)], jobs)
+                bank, o = list_at(h, z)
+                mms(bank, [(nm, 0, 2048), ("Lg", 1024 * h, 1024 * h + 1024)],
+                    [(T[bank][:, o:o + 64], T[nm][:, 128 * k:128 * k + 128], T.Lg[:, 1024 * h + k:1024 * h + 1024:16],
+                      k == 0, k == 15) for k in range(16)])
 
-        def lists_out(h):
-            vts(A("bc16", 128 * h, 128 * h + 128), A("psb%d" % h, 0, 128), 512.0, add)
+        def lists_out(h, z):
+            bank, o = list_at(h, z)
+            vts(A("bc16", 128 * h + z, 128 * h + z + 64), A(bank, o, o + 64), 512.0, add)
 
         def own_in(n):
             ps = T["psd%d" % n]
             jobs = [(ps[:, :], T.Z32[:, 0:128], T.zb[:, :], True, False)]
             for k in range(16):
                 jobs.append((ps[:, k:512:16], T.I16[:, :], T.nown[:, 32 * n:32 * n + 32], False, False))
-            mms([("psd%d" % n, 0, 512)], [("Z32", 0, 144), ("zb", 0, 512), ("I16", 0, 128), ("nown", 0, 128)], jobs)
+            mms("psd%d" % n, [("Z32", 0, 144), ("zb", 0, 512), ("I16", 0, 128), ("nown", 0, 128)], jobs)
 
         def blend_b(n):
             o = 128 * (n // 2) + 32 * (n % 2)
@@ -321,7 +300,7 @@ def rank_program(g, core, T, topo):
         def blend_c(n):
             o = 128 * (n // 2) + 64 + 32 * (n % 2)
             vtt(A("y16", 512 * n, 512 * n + 512), ind(A("W"), A("bc16", o, o + 32)), A("xb", 512 * n, 512 * n + 512), add)
-            mms([("psd%d" % n, 0, 512)], [("I16", 0, 128), ("y16", 512 * n, 512 * n + 512)],
+            mms("psd%d" % n, [("I16", 0, 128), ("y16", 512 * n, 512 * n + 512)],
                 [(T["psd%d" % n][:, :], T.I16[:, :], T.y16[:, 512 * n:512 * n + 512], False, True)])
 
         def size_d(n):
@@ -333,76 +312,105 @@ def rank_program(g, core, T, topo):
             vcopy(A("dS", 512 * n, 512 * n + 512), A("psd%d" % n))
 
         def sum_d(h):
-            jobs = []
-            for r in range(16):
-                jobs.append((T.psk[:, 64 * h:64 * h + 64], T.Z32[:, 16 - r:144 - r],
-                             T.dA[:, 4 * h:4 * h + 4, 16 * r:16 * r + 16], r == 0, r == 15))
-            mms([("psk", 0, 512)], [("Z32", 0, 144), ("dA", 4 * h, 4 * h + 4)], jobs)
+            bank = "psb1" if h else "psk"
+            mms(bank, [("Z32", 0, 144), ("dA", 4 * h, 4 * h + 4)],
+                [(T[bank][:, 0:64], T.Z32[:, 16 - r:144 - r], T.dA[:, 4 * h:4 * h + 4, 16 * r:16 * r + 16], r == 0, r == 15)
+                 for r in range(16)])
 
-        gather_links(0)
+        def scans(h):
+            bank, o = ("psb1" if h else "psk"), 64 * h
+            vscan(A("SC", o, o + 64), A("d0P", o, o + 64), A(bank, 0, 64), add, mx)
+            vscan(A("SC", 128 + o, 192 + o), A("d0Q", o, o + 64), A(bank, 0, 64), add, mn)
+
+        def room():
+            vtt(A("Y", 128 * t, 128 * t + 128), ind(A("dS"), P), A("own"), add)
+
+        def fix():
+            vcopy(ind(A(FRn, 0, 1536), A("vo16")), A("fx"))
+            lo = 640 if t == 0 else 128
+            mms("psm", [("EF", 0, 2048), (FRn, 128, 1536)],
+                [(T.psm[:, 0:(1536 - lo) // 16], T.EF[:, 128 * r:128 * r + 128], T[FRn][:, lo + r:1536:16], r == 0, r == 15)
+                 for r in range(16)])
+
         if t == 0:
-            for k in range(16):
-                z = (k + 5) % 16
-                vts(A("E5", 128 * k, 128 * k + 128), A("I5"), A("M1", z, z + 1), mul)
-        lists(0)
-        if t > 0:
-            vcopy(A("FL", 32, 88), A("psm", 0, 56))
-            if t > 1:
-                vcopy(A("FL", 0, 8 * (t - 1)), A("psm", 64, 64 + 8 * (t - 1)))
+            late_constants()
+        gather_links(0)
         vts(A("nown"), A("own"), -1.0, mul, -1088.0, add)
         gather_links(1)
         if t > 0:
-            p = t - 1
-            for s in range(1):
-                act(A("Y", 1024, 1408), A("LAND", 384 * p, 384 * p + 384), AF.Copy)
+            vcopy(A("FL", 32 if t == 1 else 0, 88), A("psm", 0, 56 if t == 1 else 88))
+        lists(0)
+        own_in(0)
+        gather_links(2)
+        if t > 0:
+            do("v", lambda: g.vector.tensor_reduce(out=T.ar[:, :], in_=T.REF[:, :], axis=AxisListType.X, op=add),
+               [("REF", 0, 8)], [("ar", 0, 1)])
+        vcopy(A("af"), A("a16"))
+        if t > 0:
+            vcopy(A("arh"), A("ar"))
+            act(A("Y", 1024, 1408), A("LAND", 384 * t - 384, 384 * t), AF.Copy)
             act(A("W", 512, 1408), ind(A("Y"), A("FL", 32, 88)), AF.Copy, scale=0.5)
             act(A("W", 0, 128 * t), ind(A("Y"), A("FL", 0, 8 * t)), AF.Copy, scale=0.5)
-        if t == 0:
-            late_constants()
-        own_in(0)
+        lists_out(0, 0)
+        lists_out(0, 64)
+        gather_links(3)
         lists(1)
-        for n in (1, 2, 3):
-            own_in(n)
-        mms([("psm", 0, 512)], [("BO", 0, 128), ("nown", 0, 128)], [(T.psm[:, 256:384], T.BO[:, :], T.nown[:, :], True, True)])
-        lists_out(0)
+        vts(A("al0"), A("vB"), 512.0, ge, 128.0, mul)
+        if t == 0:
+            vcopy(A("L", 0, 1024), A("LI"))
+            later_constants()
+        else:
+            vtt(ind(A("LO", 0, 1152), A("lo16")), A("LE"), A("ODDO"), add)
+        vtt(A("al1"), A("vB"), A("al0"), add)
+        vts(A("ODDN"), A("JR"), float(128 * t - 512), add, OD, mul)
+        vts(A("al2"), A("al1"), 384, band)
+        vts(A("ODDO"), A("JR"), float(128 * t + 896), add, OD, mul)
+        vts(A("al3"), A("al2"), 512.0, add)
+        vts(A("vp"), A("vB"), 128.0, add)
+        if not last:
+            vcopy(A("C", 128 * t, 128 * t + 128), A("a16"))
+        lists_out(1, 0)
         blend_b(0)
+        own_in(1)
+        lists_out(1, 64)
         blend_b(1)
         blend_c(0)
-        lists_out(1)
+        blend_b(2)
+        blend_b(3)
+        own_in(2)
         blend_c(1)
         size_d(0)
-        keep_d(0)
-        blend_b(2)
+        own_in(3)
         blend_c(2)
         size_d(1)
-        keep_d(1)
-        sum_d(0)
-        blend_b(3)
         blend_c(3)
+        sum_d(0)
+        mms("psm", [("BO", 0, 128), ("nown", 0, 128)], [(T.psm[:, 256:384], T.BO[:, :], T.nown[:, :], True, True)])
+        if t > 0:
+            mms("psm", [("BO", 0, 128), ("arh", 0, 1)], [(T.psm[:, 500:501], T.BO[:, :], T.arh[:, :], True, True)])
         size_d(2)
-        keep_d(2)
+        keep_d(0)
+        keep_d(1)
         size_d(3)
         sum_d(1)
-        keep_d(3)
-        act(A("u1"), A("psm", 256, 384), AF.Identity, scale=-1.0, bias=A("ak") if False else None) if False else None
-        vts(A("u1"), A("psm", 256, 384), -1.0, mul, float(t + 1 - 17408), add)
+        if t > 0:
+            vcopy(A("ai"), A("psm", 500, 501))
         vcopy(A("bt", 0, 64), A("bc16", 0, 64))
+        keep_d(2)
+        if t > 0:
+            vts(A("aj"), A("ai"), 15, band)
+        scans(0)
+        if t > 0:
+            vts(A("ak"), A("aj"), 32.0, mul)
         vcopy(A("bt", 64, 128), A("bc16", 128, 192))
-        vcopy(A("af"), A("a16"))
+        keep_d(3)
+        if t > 0:
+            vts(A("thr"), A("thr0"), A("ak"), add)
         if t == 0:
-            later_constants()
-            for k in range(16):
-                act(A("EF", 128 * k, 128 * k + 128), A("If"), AF.Copy, scale=A("OHf", k, k + 1))
             act(A("FR0", 640, 1536), ind(A("FR1", 128, 1536), A("FL", 32, 88)), AF.Copy)
             act(A("FR0", 128, 640), A("FR1", 128, 640), AF.Copy)
-        if last:
-            vts(A("LT"), A("L", 0, 1024), 0.0, lt, 1408.0, mul)
-            vtt(A("LO", 0, 1024), A("L", 0, 1024), A("LT"), add)
-        LN = "LO" if last else "L"
-        vts(A("ODDN"), A("JR"), float(128 * t - 512 + (1408 if last else 0)), add, OD, mul)
 
-        vscan(A("SC", 0, 128), A("d0P"), A("psk", 0, 128), 0.0, add, mx)
-        vscan(A("SC", 128, 256), A("d0Q"), A("psk", 0, 128), 0.0, add, mn)
+        scans(1)
         vts(A("hi"), A("SC", 15, 256, 16), MAG, add, MAG, sub)
         vtt(A("pkc", 0, 8), K15, A("SC", 15, 128, 16), sub)
         vtt(A("pkc", 8, 16), K15, A("SC", 143, 256, 16), add)
@@ -413,18 +421,20 @@ def rank_program(g, core, T, topo):
         vtt(A("REF"), A("SC", 15, 128, 16), A("thr"), gt)
         P, Q = A("po", 0, 8), A("po", 8, 16)
         act(A("sg"), ind(A("dS"), Q), AF.Sign)
+        if not last:
+            act(A("u1"), A("psm", 256, 384), AF.Identity, scale=-1.0, bias=float(t + 1 - 17408))
+        vtt(A("vo"), A("vp"), A("NREF"), mul)
         vtt(PR(0), ind(A("M1"), Q), A("bt"), mul)
         vtt(PR(1), ind(A("M1"), P), A("bt"), mul)
-        mms([("psb0", 0, 512)], [("Z1", 0, 144), ("pr", 0, 2)],
-            [(T.psb0[:, 0:16], T.Z1[:, 16 - r:144 - r], T.pr[:, 0:2, r:128:16], r == 0, r == 15) for r in range(16)])
-        vts(A("vp"), A("vB"), 128.0, add)
+        mms("psb0", [("Z1", 0, 144), ("pr", 0, 2)], to_list("psb0", 0, lambda r: T.pr[:, 0:2, r:128:16], 2))
+        vtt(A("vq"), A("vo"), LIc, add)
         vtt(PR(2), ind(A("M1"), P), A("af"), mul)
         vtt(A("nrm"), ind(A("NREF"), A("CL")), A("MKH"), mul)
-        mms([("psk", 0, 512)], [("Z1", 0, 144), ("pr", 2, 3)],
-            [(T.psk[:, 256:264], T.Z1[:, 16 - r:144 - r], T.pr[:, 2, r:128:16], r == 0, r == 15) for r in range(16)])
-        for nm in ("psb1", "psd0"):
-            mms([(nm, 0, 512)], [("BO", 0, 128), ("pr", 2, 3), ("nrm", 0, 128)],
+        mms("psk", [("Z1", 0, 144), ("pr", 2, 3)], to_list("psk", 256, lambda r: T.pr[:, 2, r:128:16], 1))
+        for nm in ("psd0", "psd1") if last else ("psd0",):
+            mms(nm, [("BO", 0, 128), ("pr", 2, 3), ("nrm", 0, 128)],
                 [(T[nm][:, 0:128], T.BO[:, :], T.pr[:, 2, :], True, False), (T[nm][:, 0:128], T.BO[:, :], T.nrm[:, :], False, True)])
+        vcopy(A("vo16"), A("vq"))
         nw = A("NEW", 128 * t, 128 * t + 128)
         vtt(nw, A("own"), A("sg"), add)
         waits("g", nw[1], [])
@@ -445,98 +455,92 @@ def rank_program(g, core, T, topo):
         g.remote_dma_fused(transfers, local_sem=T.sem["snt%d" % t])
         total["arr%d" % t] = 12
         total["snt%d" % t] = 12
-        note("r", [], [("LAND", 384 * t, 384 * t + 384)], "arr%d" % t, 12)
+        note("r", {}, [], [("LAND", 384 * t, 384 * t + 384)], "arr%d" % t, 12)
 
-        vtt(A("vo"), A("vp"), A("NREF"), mul)
-        vtt(A("vo"), A("vo"), LIc, add)
         vcopy(A("l16"), A("psb0", 0, 16))
-        vcopy(A("vo16"), A("vo"))
+        if not last:
+            vts(A("al4"), A("REF"), float(128 * t), mul)
         vcopy(A("er"), ind(A(FRc, 128, 1536), A("l16", 0, 8)))
-        vcopy(A("lamA"), A("psk", 256, 264))
-        vcopy(A("ap16"), A("psk", 256, 264))
+        if not last:
+            vtt(A("alt"), A("al3"), A("NREF"), mul)
+        act(A("lamA"), A("psk", 256, 264), AF.Copy)
         vcopy(ind(A(FRc, 0, 1536), A("vo16")), A("er"))
-        for c in range(4):
-            act(A("DD", 128 * c, 128 * c + 128), A("psd0", 0, 128), AF.Abs if False else AF.Identity, scale=-1.0,
-                bias=A("lamA", c, c + 1)) if False else None
-        for c in range(4):
+        if not last:
+            mms("psb1", [("EF", 0, 2048), ("er", 0, 128)],
+                [(T.psb1[:, 384:392], T.EF[:, 128 * r:128 * r + 128], T.er[:, r:128:16], r == 0, r == 15) for r in range(16)])
+        vcopy(A("ap16"), A("psk", 256, 264))
+        if not last:
+            vtt(A("aln"), A("alt"), A("al4"), add)
+        for c in range(4 if last else 8):
             act(A("DD", 128 * c, 128 * c + 128), A("psd0", 0, 128), AF.Abs, scale=-1.0, bias=A("lamA", c, c + 1))
-        act(A("LE"), ind(A(LN, 0, 1024), A("ap16")), AF.Copy, scale=EV)
+        act(A("LE"), ind(A("L", 0, 1024), A("ap16")), AF.Copy, scale=EV)
         act(A(FRn, 640, 1536), ind(A(FRc, 128, 1536), A("FL", 32, 88)), AF.Copy)
         if t > 0:
             act(A(FRn, 128, 128 + 128 * t), ind(A(FRc, 128, 1536), A("FL", 0, 8 * t)), AF.Copy)
         if not last:
             vtt(A("wm"), ind(A(FRc, 128, 1536), A("l16", 8, 16)), A("MK"), mul)
-            vtt(A("em"), A("er"), A("MK"), mul)
-            vscan(A("ws"), A("d0S"), A("wm"), 0.0, mul, add)
-            vscan(A("es"), A("d0S"), A("em"), 0.0, mul, add)
+            vtt(A("t0"), A("lamA"), TRc, sub)
+            vscan(A("ws"), A("d0S"), A("wm"), mul, add)
+            vtt(A("t1"), A("t0"), A("REF"), mul)
             vcopy(A("w16"), A("ws", 15, 128, 16))
-            vcopy(A("e16"), A("es", 15, 128, 16))
-            vtt(A("wm2"), ind(A(FRc, 128, 1536), A("w16")), A("MK"), mul)
-            vts(A("al0"), A("vB"), 512.0, ge, 128.0, mul)
-            vscan(A("ws2"), A("d0S"), A("wm2"), 0.0, mul, add)
-            vtt(A("al1"), A("vB"), A("al0"), add)
+            vtt(A("em"), ind(A(FRc, 128, 1536), A("w16")), A("MK"), mul)
+            vscan(A("es"), A("d0S"), A("em"), mul, add)
+            vtt(A("um"), ind(A("M1"), P), A("u1"), mul)
+            vcopy(A("wi"), A("es", 15, 128, 16))
+            vts(A("gh"), A("es", 15, 128, 16), 1024.0, ge)
+            vts(A("ng"), A("es", 15, 128, 16), 1024.0, lt)
+            vts(A("wB"), A("wi"), 1920, band)
+            vtt(A("cn"), A("um"), A("af"), add)
+            vtt(A("x1"), A("wB"), A("ng"), mul)
+            vts(A("cm"), A("cn"), 1023, band)
+            vtt(A("ga"), A("gh"), A("aln"), mul)
+            vcopy(ind(A("C"), A("v16")), A("cm"))
+            vtt(A("gb"), A("ga"), LIc, add)
+            vcopy(A("e16"), A("psb1", 384, 392))
         else:
             vtt(A("em"), A("er"), A("MK"), mul)
-            vscan(A("es"), A("d0S"), A("em"), 0.0, mul, add)
+            vtt(A("t0"), A("lamA"), TRc, sub)
+            vscan(A("es"), A("d0S"), A("em"), mul, add)
+            vtt(A("t1"), A("t0"), A("REF"), mul)
             vcopy(A("e16"), A("es", 15, 128, 16))
-        vcopy(A("fx"), ind(A(FRc, 128, 1536), A("e16")))
-        for c in range(4, 8):
-            vts(A("DD", 128 * c, 128 * c + 128), A("psb1", 0, 128), A("lamA", c, c + 1), ne)
-        vtt(A("t1"), A("lamA"), TRc, sub)
-        vscan(A("DS"), A("d0D"), A("DD"), 0.0, add, mn)
-        vtt(A("t1"), A("t1"), A("REF"), mul)
+            for c in range(4, 8):
+                vts(A("DD", 128 * c, 128 * c + 128), A("psd1", 0, 128), A("lamA", c, c + 1), ne)
+            room()
+        act(A("fx"), ind(A(FRc, 128, 1536), A("e16")), AF.Copy)
+        if t == 0:
+            act(A("LO", 0, 1024), A("L", 0, 1024), AF.Copy)
+        vscan(A("DS"), A("d0D"), A("DD"), add, mn)
+        if not last:
+            vtt(A("vf"), A("x1"), A("gb"), add)
         vtt(A("t2"), A("DS", 127, 1024, 128), TD, ge)
+        if not last:
+            vtt(A("vB"), A("x1"), A("ga"), add)
+            fix()
         vtt(A("t3"), A("t2"), A("t1"), mul)
         if not last:
-            vts(A("al2"), A("al1"), 384, AluOpType.bitwise_and)
-        vtt(A("t3"), A("t3"), TRc, add)
+            room()
+        vtt(A("t4"), A("t3"), TRc, add)
         if not last:
-            vts(A("al3"), A("al2"), 512.0, add)
-        vcopy(A("lo16"), A("t3"))
+            vcopy(ind(A("Y", 0, 1024), A("v16")), nw)
+        vcopy(A("lo16"), A("t4"))
         if not last:
-            vtt(A("alt"), A("al3"), A("NREF"), mul)
-            vts(A("al4"), A("REF"), float(128 * t), mul)
-            vcopy(A("wi"), A("ws2", 15, 128, 16))
-            vtt(A("aln"), A("alt"), A("al4"), add)
-            vts(A("gh"), A("ws2", 15, 128, 16), 1024.0, ge)
-            vts(A("wB"), A("wi"), 1920, AluOpType.bitwise_and)
-            vts(A("ng"), A("ws2", 15, 128, 16), 1024.0, lt)
-            vtt(A("ga"), A("gh"), A("aln"), mul)
-            vtt(A("x1"), A("wB"), A("ng"), mul)
-            vtt(A("gb"), A("ga"), LIc, add)
-            vtt(A("vB"), A("x1"), A("ga"), add)
-            vtt(A("vf"), A("x1"), A("gb"), add)
-        vtt((ind(A(LN, 0, 1152), A("lo16"))), A("LE"), A("ODDN"), add)
-        vtt(A("Y", 128 * t, 128 * t + 128), ind(A("dS"), P), A("own"), add)
-        vcopy(ind(A("Y", 0, 1024), A("v16")), nw)
-        if not last:
-            vtt(A("um"), ind(A("M1"), P), A("u1"), mul)
-            vcopy(A("C", 128 * t, 128 * t + 128), A("a16"))
-            vtt(A("cn"), A("um"), A("af"), add)
-            vts(A("cm"), A("cn"), 1023, AluOpType.bitwise_and)
-            vcopy(ind(A("C"), A("v16")), A("cm"))
-            do("v", lambda: g.vector.tensor_reduce(out=T.ar[:, :], in_=T.REF[:, :], axis=AxisListType.X, op=add),
-               [("REF", 0, 8)], [("ar", 0, 1)])
-            vcopy(A("arh"), A("ar"))
-            mms([("psb0", 0, 512)], [("BO", 0, 128), ("arh", 0, 1)], [(T.psb0[:, 64:65], T.BO[:, :], T.arh[:, :], True, True)])
             vcopy(A("v16"), A("vf"))
-            vcopy(A("ai"), A("psb0", 64, 65))
-            vts(A("aj"), A("ai"), 15, AluOpType.bitwise_and)
-            vts(A("ak"), A("aj"), 32.0, mul)
-            vts(A("thr"), A("thr0"), A("ak"), add)
-        FRc = FRn
+            vtt(ind(A("L", 0, 1152), A("lo16")), A("LE"), A("ODDN"), add)
+            vcopy(A("a16"), ind(A("C"), A("v16")))
+            act(A("own"), ind(A("Y", 0, 1024), A("v16")), AF.Copy)
+        else:
+            vtt(ind(A("LO", 0, 1152), A("lo16")), A("LE"), A("ODDO"), add)
+            fix()
+            vcopy(ind(A("Y", 0, 1024), A("v16")), nw)
+        FRc, FRn = FRn, FRc
 
-    dma("s", T.yo[:, 0:512], T.Y[:, 512:1024], [("Y", 512, 1024)], [], "out0")
-    dma("s", T.yo[:, 896:1408], T.Y[:, 0:512], [("Y", 0, 512)], [], "out1")
-    dma("s", T.lo[:, :], T.LO[:, 0:1024], [("LO", 0, 1024)], [], "out2")
-    vcopy(ind(A(FRc, 0, 1536), A("vo16")), A("fx"))
-    extract_f(FRc, RO - 1)
-    vts(A("FO", 80, 88), LIc, 1280.0, add)
-    vts(A("FOt", 0, 56), A("psm", 0, 56), 512.0, lt, 1408.0, mul)
-    vts(A("FOt", 56, 80), A("psm", 64, 88), 512.0, lt, 1408.0, mul)
-    vtt(A("FOt", 0, 56), A("psm", 0, 56), A("FOt", 0, 56), add)
-    vtt(A("FOt", 56, 80), A("psm", 64, 88), A("FOt", 56, 80), add)
-    vts(A("FO", 0, 80), A("FOt", 0, 80), -512.0, add)
+    dma("s", T.lo[:, :], T.LO[:, 0:1024], [("LO", 0, 1024)], [], "out0")
+    dma("s", T.yo[:, 0:512], T.Y[:, 512:1024], [("Y", 512, 1024)], [], "out1")
+    dma("s", T.yo[:, 896:1408], T.Y[:, 0:512], [("Y", 0, 512)], [], "out2")
+    vts(A("FOt"), A("psm", 0, 88), 512.0, lt, 1408.0, mul)
+    vtt(A("FOu"), A("psm", 0, 88), A("FOt"), add)
+    vts(A("FO", 0, 56), A("FOu", 32, 88), -512.0, add)
+    vts(A("FO", 56, 88), A("FOu", 0, 32), -512.0, add)
     dma("a", T.fo[:, :], T.FO[:, :], [("FO", 0, 88)], [], "out3")
     p = 384 * (RO - 1)
     dma("s", T.yo[:, 512:896], T.LAND[:, p:p + 384], [("LAND", p, p + 384)], [], "out4")

@@ -34,7 +34,7 @@ for _n, _c, _d in (
 for _n in ("psb0", "psb1", "psd0", "psd1", "psd2", "psd3", "psk", "psm"):
     SCRATCH[_n] = ("psum", [128, 512], F32)
 
-SEMAPHORES = ["dv", "ac", "pe", "gp"] + ["in%d" % i for i in range(6)] + ["out%d" % i for i in range(5)] + \
+SEMAPHORES = ["dv", "ac", "pe", "gp"] + ["in%d" % i for i in range(6)] + ["out%d" % i for i in range(6)] + \
              ["arr%d" % t for t in range(RO)] + ["snt%d" % t for t in range(RO)]
 
 
@@ -181,9 +181,9 @@ def rank_program(g, core, T, topo):
     dma("s", T.LI[:, :], T.lk[:, :], [], [("LI", 0, 1024)], "in0")
     dma("a", T.C[:, 512:640], T.cl[:, 0:128], [], [("C", 512, 640)], "in1")
     dma("a", T.FW[:, :], T.fw0[:, :], [], [("FW", 0, 56)], "in2")
+    dma("a", T.TH8[0:8, :], T.th[:, :], [], [("TH8", 0, 128)], "in5")
     dma("s", T.Y[:, 512:1408], T.y0[:, :], [], [("Y", 512, 1408)], "in3")
     dma("s", T.C[:, 640:1024], T.cl[:, 128:512], [], [("C", 640, 1024)], "in4")
-    dma("s", T.TH8[0:8, :], T.th[:, :], [], [("TH8", 0, 128)], "in5")
 
     iota(A("T1"), [[1, 128]], 128, -1)
     iota(A("SMI", 0, 1), [[0, 1]], 0, 1)
@@ -191,75 +191,67 @@ def rank_program(g, core, T, topo):
     iota(A("SMI", 32, 64), [[16, 32]], 0, 0)
     iota(A("SMI", 16, 24), [[1, 8]], 0, 0)
     iota(A8("T4"), [[1, 128]], 0, -16)
-    fill(A("Y", 0, 512), 0)
-    fill(A("W", 0, 512), 0)
-    fill(A("Z32"), 0)
     fill(A("zb"), 0)
+    iota(A("JR"), [[1, 128]], 0, 0, True)
+    fill(A("Y", 0, 512), 0)
+    fill(A("Z32"), 0)
     fill(A("d0P"), 1)
     fill(A("d0Q"), -1)
+    fill(A("W", 0, 512), 0)
     fill(A("d0S"), 1)
     fill(A("vB"), 512)
-    iota(A("JR"), [[1, 128]], 0, 0, True)
-    fill(A("C", 0, 512), 0, False)
     iota(A("FR1", 128, 1536), [[1, 1408]], 0, 0, True)
+    iota(A("FR0", 128, 640), [[1, 512]], 0, 0, True)
+    fill(A("C", 0, 512), 0, False)
 
     vts(A("T1a"), A("T1"), 15, band)
-    vts(A("T2a"), A("T2"), 4, shr)
-    vts(A("I16"), A("T1"), 128, eq)
+    vts(A("If"), A("T1"), 128, eq)
     vts(A("M1", 0, 128), A("T1a"), 0, eq)
-    vts(A("BO"), A("T2a"), 0, eq)
+    vts(A("I16"), A("T1"), 128, eq)
+    vcopy(A("OHf"), A("M1", 0, 16))
+    vcopy(A("M1", 128, 256), A("M1", 0, 128))
     vts(A("SMI", 1, 2), A("SMI", 0, 1), 15, band)
     vts(A("SMI", 2, 3), A("SMI", 0, 1), 1, band)
-    vts(A("FL", 32, 88), A("FW"), 512, add)
-    vcopy(A("M1", 128, 256), A("M1", 0, 128))
+    vts(A("T2a"), A("T2"), 4, shr)
     vcopy(RC, A("SMI", 1, 2))
+    vcopy(OD, A("SMI", 2, 3))
+    vts(A("BO"), A("T2a"), 0, eq)
     vts(A("FL", 0, 32), A("SMI", 32, 64), RC, add)
+    vts(LIc, A("SMI", 32, 40), RC, add)
     for k in range(16):
         vts(A("E", 128 * k, 128 * k + 128), A("I16"), A("M1", k, k + 1), mul)
-    vcopy(A("OHf"), A("M1", 0, 16))
-    vts(A("If"), A("T1"), 128, eq)
     vtt(A("I5"), A("M1", 5, 133), A("BO"), mul)
+    vts(A("FL", 32, 88), A("FW"), 512, add)
     vts(A("v16"), A("SMI", 32, 40), RC, add, 512, add)
     vcopy(A("a16"), A("C", 512, 640))
     for k in range(16):
         z = (k + 5) % 16
         vts(A("E5", 128 * k, 128 * k + 128), A("I5"), A("M1", z, z + 1), mul)
 
-    act(A("W", 512, 1408), ind(A("Y"), A("FL", 32, 88)), AF.Copy, scale=0.5)
-    act(A("own"), ind(A("Y", 0, 1024), A("v16")), AF.Copy)
-    for k in range(16):
-        act(A("EF", 128 * k, 128 * k + 128), A("If"), AF.Copy, scale=A("OHf", k, k + 1))
+    act(A("MK"), A("M1", 0, 128), AF.Copy)
+    act(A("MKH"), A("M1", 0, 128), AF.Copy, scale=0.5)
     for j in (256, 512, 1024):
         act(A("M1", j, 2 * j), A("M1", 0, j), AF.Copy)
+    for k in range(16):
+        act(A("EF", 128 * k, 128 * k + 128), A("If"), AF.Copy, scale=A("OHf", k, k + 1))
+    for j in (0, 512):
+        act(A("d0D", j, j + 512), A("zb"), AF.Copy, bias=-1.0 / 256)
+    act(TRc, LIc, AF.Copy, bias=1024.0)
+    act(TD, LIc, AF.Copy, scale=1.0 / 256, bias=-127.0 / 256)
+    for o, z in ((SF(3), -512.0), (SF(4), 896.0), (SF(5), 128.0)):
+        act(o, OD, AF.Copy, scale=z)
+    act(EV, OD, AF.Copy, scale=-1.0, bias=1.0)
+    act(A("ODDN"), A("JR"), AF.Identity, scale=OD, bias=SF(3))
+    act(A("ODDO"), A("JR"), AF.Identity, scale=OD, bias=SF(4))
+    act(A("own"), ind(A("Y", 0, 1024), A("v16")), AF.Copy)
+    act(A("W", 512, 1408), ind(A("Y"), A("FL", 32, 88)), AF.Copy, scale=0.5)
 
-    def late_constants():
-        vcopy(A("Z32", 16, 144, 16), A("BO", 0, 128, 16))
-        vcopy(A("Z1"), A("Z32"))
-        vts(A("Z32", 16, 144, 16), A("BO", 0, 128, 16), 32.0, mul)
-        vset(A("d0P", 0, 128, 16), -BIG)
-        vset(A("d0Q", 0, 128, 16), BIG)
-        vts(LIc, A("SMI", 32, 40), RC, add)
-        vts(K15, LIc, 16.0, mul, 15.0, add)
-
-    def later_constants():
-        vcopy(A("MK"), A("M1", 0, 128))
-        vset(A("d0S", 0, 128, 16), 0.0)
-        vts(A8("T4"), A8("T4"), 4, shr)
-        vts(A8("BT8"), A8("T4"), 0, eq)
-        vcopy(A8("THF"), A8("TH8"))
-        mms("psk", [("BT8", 0, 128), ("THF", 0, 128)], [(T.psk[:, 128:256], T.BT8[0:8, :], T.THF[0:8, :], True, True)])
-        vtt(A("em"), A("psk", 128, 256), A("MK"), mul)
-        vscan(A("es"), A("d0S"), A("em"), mul, add)
-        vts(A("thr0"), A("es", 15, 128, 16), 32.0, mul, 15.0, add)
-        vcopy(A("thr"), A("thr0"))
-        vcopy(OD, A("SMI", 2, 3))
-        vts(EV, OD, -1.0, mul, 1.0, add)
-        vts(TRc, LIc, 1024.0, add)
-        vts(TD, LIc, 1.0 / 256, mul, -127.0 / 256, add)
-        vts(A("MKH"), A("MK"), 0.5, mul)
-        vset(A("d0D"), -1.0 / 256)
-        vset(A("d0D", 0, 1024, 128), 2048.0)
-        vcopy(A("CL"), A("SMI", 16, 24))
+    vcopy(A("Z32", 16, 144, 16), A("BO", 0, 128, 16))
+    vcopy(A("Z1"), A("Z32"))
+    vts(A("Z32", 16, 144, 16), A("BO", 0, 128, 16), 32.0, mul)
+    vset(A("d0P", 0, 128, 16), -BIG)
+    vset(A("d0Q", 0, 128, 16), BIG)
+    vts(K15, LIc, 16.0, mul, 15.0, add)
 
     def to_list(bank, o, src, q):
         return [(T[bank][:, o:o + 8 * q], T.Z1[:, 16 - r:144 - r], src(r), r == 0, r == 15) for r in range(16)]
@@ -288,10 +280,8 @@ def rank_program(g, core, T, topo):
 
         def own_in(n):
             ps = T["psd%d" % n]
-            jobs = [(ps[:, :], T.Z32[:, 0:128], T.zb[:, :], True, False)]
-            for k in range(16):
-                jobs.append((ps[:, k:512:16], T.I16[:, :], T.nown[:, 32 * n:32 * n + 32], False, False))
-            mms("psd%d" % n, [("Z32", 0, 144), ("zb", 0, 512), ("I16", 0, 128), ("nown", 0, 128)], jobs)
+            mms("psd%d" % n, [("I16", 0, 128), ("nown", 0, 128)],
+                [(ps[:, k:512:16], T.I16[:, :], T.nown[:, 32 * n:32 * n + 32], k == 0, False) for k in range(16)])
 
         def blend_b(n):
             o = 128 * (n // 2) + 32 * (n % 2)
@@ -304,9 +294,7 @@ def rank_program(g, core, T, topo):
                 [(T["psd%d" % n][:, :], T.I16[:, :], T.y16[:, 512 * n:512 * n + 512], False, True)])
 
         def size_d(n):
-            for c in (0, 1):
-                act((T.dA[:, 2 * n + c, :], [("dA", 2 * n + c, 2 * n + c + 1)], []),
-                    A("psd%d" % n, 256 * c, 256 * c + 256), AF.Abs)
+            act((T.dA[:, 2 * n:2 * n + 2, :], [("dA", 2 * n, 2 * n + 2)], []), A("psd%d" % n), AF.Abs)
 
         def keep_d(n):
             vcopy(A("dS", 512 * n, 512 * n + 512), A("psd%d" % n))
@@ -332,12 +320,15 @@ def rank_program(g, core, T, topo):
                 [(T.psm[:, 0:(1536 - lo) // 16], T.EF[:, 128 * r:128 * r + 128], T[FRn][:, lo + r:1536:16], r == 0, r == 15)
                  for r in range(16)])
 
-        if t == 0:
-            late_constants()
         gather_links(0)
         vts(A("nown"), A("own"), -1.0, mul, -1088.0, add)
         gather_links(1)
-        if t > 0:
+        if t == 0:
+            vts(A8("T4"), A8("T4"), 4, shr)
+            vset(A("d0S", 0, 128, 16), 0.0)
+            vcopy(A("CL"), A("SMI", 16, 24))
+            vts(A8("BT8"), A8("T4"), 0, eq)
+        else:
             vcopy(A("FL", 32 if t == 1 else 0, 88), A("psm", 0, 56 if t == 1 else 88))
         lists(0)
         own_in(0)
@@ -358,40 +349,44 @@ def rank_program(g, core, T, topo):
         vts(A("al0"), A("vB"), 512.0, ge, 128.0, mul)
         if t == 0:
             vcopy(A("L", 0, 1024), A("LI"))
-            later_constants()
+            vcopy(A8("THF"), A8("TH8"))
+            mms("psk", [("BT8", 0, 128), ("THF", 0, 128)], [(T.psk[:, 128:256], T.BT8[0:8, :], T.THF[0:8, :], True, True)])
         else:
             vtt(ind(A("LO", 0, 1152), A("lo16")), A("LE"), A("ODDO"), add)
-        vtt(A("al1"), A("vB"), A("al0"), add)
-        vts(A("ODDN"), A("JR"), float(128 * t - 512), add, OD, mul)
-        vts(A("al2"), A("al1"), 384, band)
-        vts(A("ODDO"), A("JR"), float(128 * t + 896), add, OD, mul)
-        vts(A("al3"), A("al2"), 512.0, add)
-        vts(A("vp"), A("vB"), 128.0, add)
-        if not last:
-            vcopy(A("C", 128 * t, 128 * t + 128), A("a16"))
         lists_out(1, 0)
         blend_b(0)
         own_in(1)
-        lists_out(1, 64)
         blend_b(1)
         blend_c(0)
+        lists_out(1, 64)
+        if t == 0:
+            vtt(A("em"), A("psk", 128, 256), A("MK"), mul)
         blend_b(2)
         blend_b(3)
         own_in(2)
         blend_c(1)
+        if t == 0:
+            vscan(A("es"), A("d0S"), A("em"), mul, add)
         size_d(0)
         own_in(3)
         blend_c(2)
+        if t == 0:
+            vts(A("thr0"), A("es", 15, 128, 16), 32.0, mul, 15.0, add)
         size_d(1)
         blend_c(3)
-        sum_d(0)
+        vts(A("vp"), A("vB"), 128.0, add)
+        if t == 0:
+            vcopy(A("thr"), A("thr0"))
+            vset(A("d0D", 0, 1024, 128), 2048.0)
         mms("psm", [("BO", 0, 128), ("nown", 0, 128)], [(T.psm[:, 256:384], T.BO[:, :], T.nown[:, :], True, True)])
         if t > 0:
             mms("psm", [("BO", 0, 128), ("arh", 0, 1)], [(T.psm[:, 500:501], T.BO[:, :], T.arh[:, :], True, True)])
         size_d(2)
+        sum_d(0)
         keep_d(0)
         keep_d(1)
         size_d(3)
+        act(A("dS", 1536, 2048), A("psd3"), AF.Copy)
         sum_d(1)
         if t > 0:
             vcopy(A("ai"), A("psm", 500, 501))
@@ -403,17 +398,17 @@ def rank_program(g, core, T, topo):
         if t > 0:
             vts(A("ak"), A("aj"), 32.0, mul)
         vcopy(A("bt", 64, 128), A("bc16", 128, 192))
-        keep_d(3)
         if t > 0:
             vts(A("thr"), A("thr0"), A("ak"), add)
         if t == 0:
             act(A("FR0", 640, 1536), ind(A("FR1", 128, 1536), A("FL", 32, 88)), AF.Copy)
-            act(A("FR0", 128, 640), A("FR1", 128, 640), AF.Copy)
 
         scans(1)
+        vtt(A("al1"), A("vB"), A("al0"), add)
         vts(A("hi"), A("SC", 15, 256, 16), MAG, add, MAG, sub)
         vtt(A("pkc", 0, 8), K15, A("SC", 15, 128, 16), sub)
         vtt(A("pkc", 8, 16), K15, A("SC", 143, 256, 16), add)
+        vts(A("al2"), A("al1"), 384, band)
         vtt(A("of", 0, 8), A("pkc", 0, 8), A("hi", 0, 8), add)
         vtt(A("of", 8, 16), A("pkc", 8, 16), A("hi", 8, 16), sub)
         vtt(A("NREF"), A("SC", 15, 128, 16), A("thr"), le)
@@ -423,6 +418,9 @@ def rank_program(g, core, T, topo):
         act(A("sg"), ind(A("dS"), Q), AF.Sign)
         if not last:
             act(A("u1"), A("psm", 256, 384), AF.Identity, scale=-1.0, bias=float(t + 1 - 17408))
+        if t > 0:
+            act(A("ODDN"), A("ODDN"), AF.Identity, bias=SF(5))
+            act(A("ODDO"), A("ODDO"), AF.Identity, bias=SF(5))
         vtt(A("vo"), A("vp"), A("NREF"), mul)
         vtt(PR(0), ind(A("M1"), Q), A("bt"), mul)
         vtt(PR(1), ind(A("M1"), P), A("bt"), mul)
@@ -457,11 +455,13 @@ def rank_program(g, core, T, topo):
         total["snt%d" % t] = 12
         note("r", {}, [], [("LAND", 384 * t, 384 * t + 384)], "arr%d" % t, 12)
 
+        vts(A("al3"), A("al2"), 512.0, add)
         vcopy(A("l16"), A("psb0", 0, 16))
         if not last:
             vts(A("al4"), A("REF"), float(128 * t), mul)
         vcopy(A("er"), ind(A(FRc, 128, 1536), A("l16", 0, 8)))
         if not last:
+            vcopy(A("C", 128 * t, 128 * t + 128), A("a16"))
             vtt(A("alt"), A("al3"), A("NREF"), mul)
         act(A("lamA"), A("psk", 256, 264), AF.Copy)
         vcopy(ind(A(FRc, 0, 1536), A("vo16")), A("er"))
@@ -509,6 +509,7 @@ def rank_program(g, core, T, topo):
         act(A("fx"), ind(A(FRc, 128, 1536), A("e16")), AF.Copy)
         if t == 0:
             act(A("LO", 0, 1024), A("L", 0, 1024), AF.Copy)
+            dma("s", T.lo[0:128:2, :], T.LO[0:128:2, 0:1024], [("LO", 0, 1024)], [], "out0")
         vscan(A("DS"), A("d0D"), A("DD"), add, mn)
         if not last:
             vtt(A("vf"), A("x1"), A("gb"), add)
@@ -534,7 +535,7 @@ def rank_program(g, core, T, topo):
             vcopy(ind(A("Y", 0, 1024), A("v16")), nw)
         FRc, FRn = FRn, FRc
 
-    dma("s", T.lo[:, :], T.LO[:, 0:1024], [("LO", 0, 1024)], [], "out0")
+    dma("s", T.lo[1:128:2, :], T.LO[1:128:2, 0:1024], [("LO", 0, 1024)], [], "out5")
     dma("s", T.yo[:, 0:512], T.Y[:, 512:1024], [("Y", 512, 1024)], [], "out1")
     dma("s", T.yo[:, 896:1408], T.Y[:, 0:512], [("Y", 0, 512)], [], "out2")
     vts(A("FOt"), A("psm", 0, 88), 512.0, lt, 1408.0, mul)

from concourse.bass import DstId, RemoteDMATransfer
from concourse.mybir import AluOpType, AxisListType, ActivationFunctionType

RO = 4
BIG = 262144.0
MAG = 402653184.0
F32, BF, I32, U16, F16 = "float32", "bfloat16", "int32", "uint16", "float16"

SCRATCH = {}
for _n, _c, _d in (
        ("Y", 1408, BF), ("C", 1024, I32), ("LI", 1024, I32), ("L", 1152, F32), ("LO", 1152, F32),
        ("FW", 56, I32), ("FL", 88, U16), ("FR0", 1536, F32), ("FR1", 1536, F32), ("W", 1408, BF), ("TH8", 128, I32),
        ("THF", 128, F32), ("BT8", 128, F32), ("T4", 128, I32), ("NEW", 512, BF), ("LAND", 1536, BF),
        ("a16", 128, U16), ("af", 128, F32), ("Lg", 2048, F16), ("bc16", 256, U16), ("bt", 128, F32),
        ("xb", 2048, F32), ("y16", 2048, F16), ("dS", 2048, BF), ("dA", [8, 256], BF),
        ("own", 128, BF), ("nown", 128, F16), ("u1", 128, F32), ("SC", 256, F32), ("hi", 16, F32), ("pkc", 16, F32),
        ("of", 16, F32), ("po", 16, U16), ("pr", [3, 128], F16), ("nrm", 128, F16), ("sg", 128, BF),
        ("l16", 16, U16), ("er", 128, F32), ("em", 128, F32), ("es", 128, F32), ("e16", 8, U16), ("fx", 128, F32),
        ("wm", 128, F32), ("ws", 128, F32), ("w16", 8, U16),
        ("lamA", 8, F32), ("ap16", 8, U16), ("DD", 1024, BF), ("DS", 1024, BF), ("LE", 128, F32), ("ODDN", 128, F32),
        ("ODDO", 128, F32), ("um", 128, F32), ("cn", 128, I32), ("cm", 128, I32),
        ("REF", 8, F32), ("NREF", 8, F32), ("thr", 8, F32), ("thr0", 8, F32), ("ar", 1, F32), ("arh", 1, F16), ("ai", 1, I32),
        ("aj", 1, I32), ("ak", 1, F32), ("vB", 8, F32), ("v16", 8, U16), ("vf", 8, F32), ("vo", 8, F32), ("vq", 8, F32),
        ("vp", 8, F32), ("vo16", 8, U16), ("t0", 8, F32), ("t1", 8, F32), ("t2", 8, F32), ("t3", 8, F32), ("t4", 8, F32),
        ("lo16", 8, U16), ("al0", 8, F32), ("al1", 8, I32), ("al2", 8, I32), ("al3", 8, F32), ("al4", 8, F32), ("alt", 8, F32),
        ("aln", 8, F32), ("wi", 8, I32), ("wB", 8, I32), ("gh", 8, F32), ("ng", 8, F32), ("x1", 8, F32), ("ga", 8, F32),
        ("gb", 8, F32), ("FO", 88, F32), ("FOt", 88, F32), ("FOu", 88, F32),
        ("T1", 128, I32), ("T1a", 128, I32), ("T2", 128, I32), ("T2a", 128, I32), ("M1", 2048, BF), ("I16", 128, F16),
        ("If", 128, F32), ("BO", 128, F16), ("I5", 128, F16), ("E", 2048, F16), ("E5", 2048, F16), ("EF", 2048, F32),
        ("OHf", 16, F32), ("Z32", 144, BF), ("Z1", 144, F16), ("zb", 512, BF), ("MK", 128, F32), ("MKH", 128, F32),
        ("d0P", 128, F32), ("d0Q", 128, F32), ("d0S", 128, F32), ("d0D", 1024, BF), ("JR", 128, F32),
        ("SMI", 64, I32), ("SMF", 64, F32), ("CL", 8, U16)):
    SCRATCH[_n] = ("sbuf", [128] + (_c if isinstance(_c, list) else [_c]), _d)
for _n in ("psb0", "psb1", "psd0", "psd1", "psd2", "psd3", "psk", "psm"):
    SCRATCH[_n] = ("psum", [128, 512], F32)

SEMAPHORES = ["dv", "ac", "pe", "gp"] + ["in%d" % i for i in range(6)] + ["out%d" % i for i in range(6)] + \
             ["arr%d" % t for t in range(RO)] + ["snt%d" % t for t in range(RO)]


def rank_program(g, core, T, topo):
    rank = T.rank_of(core)
    if rank is None:
        return
    cores = T.cores
    add, sub, mul, mx, mn = AluOpType.add, AluOpType.subtract, AluOpType.mult, AluOpType.max, AluOpType.min
    ge, gt, le, lt, eq, ne = (AluOpType.is_ge, AluOpType.is_gt, AluOpType.is_le, AluOpType.is_lt, AluOpType.is_equal,
                              AluOpType.not_equal)
    band, shr = AluOpType.bitwise_and, AluOpType.arith_shift_right
    AF = ActivationFunctionType
    queues = {"v": g.vector, "a": g.scalar, "p": g.tensor, "g": g, "s": g.sync}
    semof = {"v": "dv", "a": "ac", "p": "pe", "g": "gp"}
    count = {"dv": 0, "ac": 0, "pe": 0, "gp": 0}
    known = {"v": {}, "a": {}, "p": {}, "g": {}, "s": {}}
    log = {}
    total = {}

    def waits(e, reads, writes):
        need = {}
        for toks, wr in ((reads, False), (writes, True)):
            for nm, lo, hi in toks:
                ps = nm[:2] == "ps"
                for ent in log.get(nm, []):
                    if ps:
                        if ent[3] == e:
                            continue
                    elif ent[1] <= lo or ent[0] >= hi or not (wr or ent[2]):
                        continue
                    if ent[4] not in need or need[ent[4]][0] < ent[5]:
                        need[ent[4]] = (ent[5], ent[6])
        for sem in sorted(need, key=lambda s: -len(need[s][1])):
            val, clk = need[sem]
            k = known[e]
            if k.get(sem, 0) >= val:
                continue
            queues[e].wait_ge(T.sem[sem], val)
            k[sem] = val
            for s2 in clk:
                if k.get(s2, 0) < clk[s2]:
                    k[s2] = clk[s2]

    def note(e, clk, reads, writes, sem, val):
        for toks, wr in ((reads, False), (writes, True)):
            for nm, lo, hi in toks:
                ents = log.setdefault(nm, [])
                if nm[:2] == "ps":
                    ents[:] = []
                elif wr:
                    ents[:] = [x for x in ents if not (x[0] >= lo and x[1] <= hi)]
                ents.append((lo, hi, wr, e, sem, val, clk))

    def do(e, fn, reads, writes):
        waits(e, reads, writes)
        sem = semof[e]
        count[sem] += 1
        fn().then_inc(T.sem[sem], 1)
        note(e, dict(known[e]), reads, writes, sem, count[sem])

    def dma(e, out, in_, reads, writes, sem):
        waits(e, reads, writes)
        queues[e].dma_start(out=out, in_=in_).then_inc(T.sem[sem], 16)
        total[sem] = 16
        note("d", dict(known[e]), reads, writes, sem, 16)

    def A(nm, lo=0, hi=None, st=1):
        if hi is None:
            hi = SCRATCH[nm][1][1]
        ap = T[nm][:, lo:hi] if st == 1 else T[nm][:, lo:hi:st]
        return (ap, [(nm, lo, hi)], [])

    def A8(nm):
        return (T[nm][0:8, :], [(nm, 0, 128)], [])

    def PR(q):
        return (T.pr[:, q, :], [("pr", q, q + 1)], [])

    def ind(win, off):
        return (win[0].indirect(off[0]), win[1], off[1])

    def vcopy(o, x):
        do("v", lambda: g.vector.tensor_copy(out=o[0], in_=x[0]), x[1] + x[2] + o[2], o[1])

    def vtt(o, x, y, op):
        do("v", lambda: g.vector.tensor_tensor(out=o[0], in0=x[0], in1=y[0], op=op), x[1] + x[2] + y[1] + o[2], o[1])

    def vts(o, x, s1, op0, s2=None, op1=None):
        rd = x[1] + x[2] + o[2]
        a1, a2 = s1, s2
        if isinstance(s1, tuple):
            rd = rd + s1[1]
            a1 = s1[0]
        if isinstance(s2, tuple):
            rd = rd + s2[1]
            a2 = s2[0]
        if op1 is None:
            do("v", lambda: g.vector.tensor_scalar(out=o[0], in0=x[0], scalar1=a1, scalar2=None, op0=op0), rd, o[1])
        else:
            do("v", lambda: g.vector.tensor_scalar(out=o[0], in0=x[0], scalar1=a1, scalar2=a2, op0=op0, op1=op1), rd, o[1])

    def vscan(o, d0, d1, op0, op1):
        do("v", lambda: g.vector.tensor_tensor_scan(out=o[0], data0=d0[0], data1=d1[0], initial=0.0, op0=op0, op1=op1),
           d0[1] + d1[1], o[1])

    def vset(o, c):
        do("v", lambda: g.vector.memset(o[0], c), [], o[1])

    def act(o, x, f, bias=None, scale=None):
        rd = x[1] + x[2]
        kw = {}
        for key, z in (("bias", bias), ("scale", scale)):
            if isinstance(z, tuple):
                rd = rd + z[1]
                kw[key] = z[0]
            elif z is not None:
                kw[key] = z
        do("a", lambda: g.scalar.activation(out=o[0], in_=x[0], func=f, **kw), rd, o[1])

    def mms(bank, reads, jobs):
        def fn():
            last = None
            for o, l, r, st, sp in jobs:
                last = g.tensor.matmul(out=o, lhsT=l, rhs=r, start=st, stop=sp)
            return last
        do("p", fn, reads, [(bank, 0, 512)])

    def iota(o, pattern, base, cmul, flag=False):
        if flag:
            do("g", lambda: g.iota(o[0], pattern=pattern, base=base, channel_multiplier=cmul,
                                   allow_small_or_imprecise_dtypes=True), [], o[1])
        else:
            do("g", lambda: g.iota(o[0], pattern=pattern, base=base, channel_multiplier=cmul), [], o[1])

    def fill(o, c, flag=True):
        iota(o, [[0, o[1][0][2] - o[1][0][1]]], c, 0, flag)

    def SF(j, n=1):
        return A("SMF", j, j + n)

    RC, EV, OD, LIc, K15, TRc, TD = SF(0), SF(1), SF(2), SF(8, 8), SF(16, 8), SF(24, 8), SF(32, 8)

    dma("s", T.LI[:, :], T.lk[:, :], [], [("LI", 0, 1024)], "in0")
    dma("a", T.C[:, 512:640], T.cl[:, 0:128], [], [("C", 512, 640)], "in1")
    dma("a", T.FW[:, :], T.fw0[:, :], [], [("FW", 0, 56)], "in2")
    dma("a", T.TH8[0:8, :], T.th[:, :], [], [("TH8", 0, 128)], "in5")
    dma("s", T.Y[:, 512:1408], T.y0[:, :], [], [("Y", 512, 1408)], "in3")
    dma("s", T.C[:, 640:1024], T.cl[:, 128:512], [], [("C", 640, 1024)], "in4")

    iota(A("T1"), [[1, 128]], 128, -1)
    iota(A("SMI", 0, 1), [[0, 1]], 0, 1)
    iota(A("T2"), [[16, 8], [0, 16]], 15, -1)
    iota(A("SMI", 32, 64), [[16, 32]], 0, 0)
    iota(A("SMI", 16, 24), [[1, 8]], 0, 0)
    iota(A8("T4"), [[1, 128]], 0, -16)
    fill(A("zb"), 0)
    iota(A("JR"), [[1, 128]], 0, 0, True)
    fill(A("Y", 0, 512), 0)
    fill(A("Z32"), 0)
    fill(A("d0P"), 1)
    fill(A("d0Q"), -1)
    fill(A("W", 0, 512), 0)
    fill(A("d0S"), 1)
    fill(A("vB"), 512)
    iota(A("FR1", 128, 1536), [[1, 1408]], 0, 0, True)
    iota(A("FR0", 128, 640), [[1, 512]], 0, 0, True)
    fill(A("C", 0, 512), 0, False)

    vts(A("T1a"), A("T1"), 15, band)
    vts(A("If"), A("T1"), 128, eq)
    vts(A("M1", 0, 128), A("T1a"), 0, eq)
    vts(A("I16"), A("T1"), 128, eq)
    vcopy(A("OHf"), A("M1", 0, 16))
    vcopy(A("M1", 128, 256), A("M1", 0, 128))
    vts(A("SMI", 1, 2), A("SMI", 0, 1), 15, band)
    vts(A("SMI", 2, 3), A("SMI", 0, 1), 1, band)
    vts(A("T2a"), A("T2"), 4, shr)
    vcopy(RC, A("SMI", 1, 2))
    vcopy(OD, A("SMI", 2, 3))
    vts(A("BO"), A("T2a"), 0, eq)
    vts(A("FL", 0, 32), A("SMI", 32, 64), RC, add)
    vts(LIc, A("SMI", 32, 40), RC, add)
    for k in range(16):
        vts(A("E", 128 * k, 128 * k + 128), A("I16"), A("M1", k, k + 1), mul)
    vtt(A("I5"), A("M1", 5, 133), A("BO"), mul)
    vts(A("FL", 32, 88), A("FW"), 512, add)
    vts(A("v16"), A("SMI", 32, 40), RC, add, 512, add)
    vcopy(A("a16"), A("C", 512, 640))
    for k in range(16):
        z = (k + 5) % 16
        vts(A("E5", 128 * k, 128 * k + 128), A("I5"), A("M1", z, z + 1), mul)

    act(A("MK"), A("M1", 0, 128), AF.Copy)
    act(A("MKH"), A("M1", 0, 128), AF.Copy, scale=0.5)
    for j in (256, 512, 1024):
        act(A("M1", j, 2 * j), A("M1", 0, j), AF.Copy)
    for k in range(16):
        act(A("EF", 128 * k, 128 * k + 128), A("If"), AF.Copy, scale=A("OHf", k, k + 1))
    for j in (0, 512):
        act(A("d0D", j, j + 512), A("zb"), AF.Copy, bias=-1.0 / 256)
    act(TRc, LIc, AF.Copy, bias=1024.0)
    act(TD, LIc, AF.Copy, scale=1.0 / 256, bias=-127.0 / 256)
    for o, z in ((SF(3), -512.0), (SF(4), 896.0), (SF(5), 128.0)):
        act(o, OD, AF.Copy, scale=z)
    act(EV, OD, AF.Copy, scale=-1.0, bias=1.0)
    act(A("ODDN"), A("JR"), AF.Identity, scale=OD, bias=SF(3))
    act(A("ODDO"), A("JR"), AF.Identity, scale=OD, bias=SF(4))
    act(A("own"), ind(A("Y", 0, 1024), A("v16")), AF.Copy)
    act(A("W", 512, 1408), ind(A("Y"), A("FL", 32, 88)), AF.Copy, scale=0.5)

    vcopy(A("Z32", 16, 144, 16), A("BO", 0, 128, 16))
    vcopy(A("Z1"), A("Z32"))
    vts(A("Z32", 16, 144, 16), A("BO", 0, 128, 16), 32.0, mul)
    vset(A("d0P", 0, 128, 16), -BIG)
    vset(A("d0Q", 0, 128, 16), BIG)
    vts(K15, LIc, 16.0, mul, 15.0, add)

    def to_list(bank, o, src, q):
        return [(T[bank][:, o:o + 8 * q], T.Z1[:, 16 - r:144 - r], src(r), r == 0, r == 15) for r in range(16)]

    FRc, FRn = "FR0", "FR1"
    for t in range(RO):
        last = t == RO - 1

        def gather_links(q):
            src = A("LI") if t == 0 else A("L", 0, 1024)
            vcopy(A("Lg", 512 * q, 512 * q + 512), ind(src, A("a16", 32 * q, 32 * q + 32)))

        def list_at(h, z):
            return ("psm", 400) if h and z else ("psb%d" % h, z)

        def lists(h):
            for z, nm in ((0, "E"), (64, "E5")):
                bank, o = list_at(h, z)
                mms(bank, [(nm, 0, 2048), ("Lg", 1024 * h, 1024 * h + 1024)],
                    [(T[bank][:, o:o + 64], T[nm][:, 128 * k:128 * k + 128], T.Lg[:, 1024 * h + k:1024 * h + 1024:16],
                      k == 0, k == 15) for k in range(16)])

        def lists_out(h, z):
            bank, o = list_at(h, z)
            vts(A("bc16", 128 * h + z, 128 * h + z + 64), A(bank, o, o + 64), 512.0, add)

        def own_in(n):
            ps = T["psd%d" % n]
            mms("psd%d" % n, [("I16", 0, 128), ("nown", 0, 128)],
                [(ps[:, k:512:16], T.I16[:, :], T.nown[:, 32 * n:32 * n + 32], k == 0, False) for k in range(16)])

        def blend_b(n):
            o = 128 * (n // 2) + 32 * (n % 2)
            act(A("xb", 512 * n, 512 * n + 512), ind(A("W"), A("bc16", o, o + 32)), AF.Copy, bias=1087.75)

        def blend_c(n):
            o = 128 * (n // 2) + 64 + 32 * (n % 2)
            vtt(A("y16", 512 * n, 512 * n + 512), ind(A("W"), A("bc16", o, o + 32)), A("xb", 512 * n, 512 * n + 512), add)
            mms("psd%d" % n, [("I16", 0, 128), ("y16", 512 * n, 512 * n + 512)],
                [(T["psd%d" % n][:, :], T.I16[:, :], T.y16[:, 512 * n:512 * n + 512], False, True)])

        def size_d(n):
            act((T.dA[:, 2 * n:2 * n + 2, :], [("dA", 2 * n, 2 * n + 2)], []), A("psd%d" % n), AF.Abs)

        def keep_d(n):
            vcopy(A("dS", 512 * n, 512 * n + 512), A("psd%d" % n))

        def sum_d(h):
            bank = "psb1" if h else "psk"
            mms(bank, [("Z32", 0, 144), ("dA", 4 * h, 4 * h + 4)],
                [(T[bank][:, 0:64], T.Z32[:, 16 - r:144 - r], T.dA[:, 4 * h:4 * h + 4, 16 * r:16 * r + 16], r == 0, r == 15)
                 for r in range(16)])

        def scans(h):
            bank, o = ("psb1" if h else "psk"), 64 * h
            vscan(A("SC", o, o + 64), A("d0P", o, o + 64), A(bank, 0, 64), add, mx)
            vscan(A("SC", 128 + o, 192 + o), A("d0Q", o, o + 64), A(bank, 0, 64), add, mn)

        def room():
            vtt(A("Y", 128 * t, 128 * t + 128), ind(A("dS"), P), A("own"), add)

        def fix():
            vcopy(ind(A(FRn, 0, 1536), A("vo16")), A("fx"))
            lo = 640 if t == 0 else 128
            mms("psm", [("EF", 0, 2048), (FRn, 128, 1536)],
                [(T.psm[:, 0:(1536 - lo) // 16], T.EF[:, 128 * r:128 * r + 128], T[FRn][:, lo + r:1536:16], r == 0, r == 15)
                 for r in range(16)])

        gather_links(0)
        vts(A("nown"), A("own"), -1.0, mul, -1088.0, add)
        gather_links(1)
        if t == 0:
            vts(A8("T4"), A8("T4"), 4, shr)
            vset(A("d0S", 0, 128, 16), 0.0)
            vcopy(A("CL"), A("SMI", 16, 24))
            vts(A8("BT8"), A8("T4"), 0, eq)
        else:
            vcopy(A("FL", 32 if t == 1 else 0, 88), A("psm", 0, 56 if t == 1 else 88))
        lists(0)
        own_in(0)
        gather_links(2)
        if t > 0:
            do("v", lambda: g.vector.tensor_reduce(out=T.ar[:, :], in_=T.REF[:, :], axis=AxisListType.X, op=add),
               [("REF", 0, 8)], [("ar", 0, 1)])
        vcopy(A("af"), A("a16"))
        if t > 0:
            vcopy(A("arh"), A("ar"))
            act(A("Y", 1024, 1408), A("LAND", 384 * t - 384, 384 * t), AF.Copy)
            act(A("W", 512, 1408), ind(A("Y"), A("FL", 32, 88)), AF.Copy, scale=0.5)
            act(A("W", 0, 128 * t), ind(A("Y"), A("FL", 0, 8 * t)), AF.Copy, scale=0.5)
        lists_out(0, 0)
        lists_out(0, 64)
        gather_links(3)
        lists(1)
        vts(A("al0"), A("vB"), 512.0, ge, 128.0, mul)
        if t == 0:
            vcopy(A("L", 0, 1024), A("LI"))
            vcopy(A8("THF"), A8("TH8"))
            mms("psk", [("BT8", 0, 128), ("THF", 0, 128)], [(T.psk[:, 128:256], T.BT8[0:8, :], T.THF[0:8, :], True, True)])
        else:
            vtt(ind(A("LO", 0, 1152), A("lo16")), A("LE"), A("ODDO"), add)
        lists_out(1, 0)
        blend_b(0)
        own_in(1)
        blend_b(1)
        blend_c(0)
        lists_out(1, 64)
        if t == 0:
            vtt(A("em"), A("psk", 128, 256), A("MK"), mul)
        blend_b(2)
        blend_b(3)
        own_in(2)
        blend_c(1)
        if t == 0:
            vscan(A("es"), A("d0S"), A("em"), mul, add)
        size_d(0)
        own_in(3)
        blend_c(2)
        if t == 0:
            vts(A("thr0"), A("es", 15, 128, 16), 32.0, mul, 15.0, add)
        size_d(1)
        blend_c(3)
        vts(A("vp"), A("vB"), 128.0, add)
        if t == 0:
            vcopy(A("thr"), A("thr0"))
            vset(A("d0D", 0, 1024, 128), 2048.0)
        mms("psm", [("BO", 0, 128), ("nown", 0, 128)], [(T.psm[:, 256:384], T.BO[:, :], T.nown[:, :], True, True)])
        if t > 0:
            mms("psm", [("BO", 0, 128), ("arh", 0, 1)], [(T.psm[:, 500:501], T.BO[:, :], T.arh[:, :], True, True)])
        size_d(2)
        sum_d(0)
        keep_d(0)
        keep_d(1)
        size_d(3)
        act(A("dS", 1536, 2048), A("psd3"), AF.Copy)
        sum_d(1)
        if t > 0:
            vcopy(A("ai"), A("psm", 500, 501))
        vcopy(A("bt", 0, 64), A("bc16", 0, 64))
        keep_d(2)
        if t > 0:
            vts(A("aj"), A("ai"), 15, band)
        scans(0)
        if t > 0:
            vts(A("ak"), A("aj"), 32.0, mul)
        vcopy(A("bt", 64, 128), A("bc16", 128, 192))
        if t > 0:
            vts(A("thr"), A("thr0"), A("ak"), add)
        if t == 0:
            act(A("FR0", 640, 1536), ind(A("FR1", 128, 1536), A("FL", 32, 88)), AF.Copy)

        scans(1)
        vtt(A("al1"), A("vB"), A("al0"), add)
        vts(A("hi"), A("SC", 15, 256, 16), MAG, add, MAG, sub)
        vtt(A("pkc", 0, 8), K15, A("SC", 15, 128, 16), sub)
        vtt(A("pkc", 8, 16), K15, A("SC", 143, 256, 16), add)
        vts(A("al2"), A("al1"), 384, band)
        vtt(A("of", 0, 8), A("pkc", 0, 8), A("hi", 0, 8), add)
        vtt(A("of", 8, 16), A("pkc", 8, 16), A("hi", 8, 16), sub)
        vtt(A("NREF"), A("SC", 15, 128, 16), A("thr"), le)
        vcopy(A("po"), A("of"))
        vtt(A("REF"), A("SC", 15, 128, 16), A("thr"), gt)
        P, Q = A("po", 0, 8), A("po", 8, 16)
        act(A("sg"), ind(A("dS"), Q), AF.Sign)
        if not last:
            act(A("u1"), A("psm", 256, 384), AF.Identity, scale=-1.0, bias=float(t + 1 - 17408))
        if t > 0:
            act(A("ODDN"), A("ODDN"), AF.Identity, bias=SF(5))
            act(A("ODDO"), A("ODDO"), AF.Identity, bias=SF(5))
        vtt(A("vo"), A("vp"), A("NREF"), mul)
        vtt(PR(0), ind(A("M1"), Q), A("bt"), mul)
        vtt(PR(1), ind(A("M1"), P), A("bt"), mul)
        mms("psb0", [("Z1", 0, 144), ("pr", 0, 2)], to_list("psb0", 0, lambda r: T.pr[:, 0:2, r:128:16], 2))
        vtt(A("vq"), A("vo"), LIc, add)
        vtt(PR(2), ind(A("M1"), P), A("af"), mul)
        vtt(A("nrm"), ind(A("NREF"), A("CL")), A("MKH"), mul)
        mms("psk", [("Z1", 0, 144), ("pr", 2, 3)], to_list("psk", 256, lambda r: T.pr[:, 2, r:128:16], 1))
        for nm in ("psd0", "psd1") if last else ("psd0",):
            mms(nm, [("BO", 0, 128), ("pr", 2, 3), ("nrm", 0, 128)],
                [(T[nm][:, 0:128], T.BO[:, :], T.pr[:, 2, :], True, False), (T[nm][:, 0:128], T.BO[:, :], T.nrm[:, :], False, True)])
        vcopy(A("vo16"), A("vq"))
        nw = A("NEW", 128 * t, 128 * t + 128)
        vtt(nw, A("own"), A("sg"), add)
        waits("g", nw[1], [])
        used, transfers = set(), []
        others = sorted([c for c in cores if c != core], key=lambda c: len(topo.engines(core, c)))
        for c in others:
            fewest = topo.engines(core, others[0])
            eng = [e for e in topo.engines(core, c) if e not in used]
            if len(topo.engines(core, c)) > len(fewest):
                eng = [e for e in eng if e not in fewest]
            eng = eng[:4]
            used.update(eng)
            s = (rank - T.rank_of(c) - 1) % len(cores)
            rid, pid = topo.addr(c, core)
            transfers.append(RemoteDMATransfer(dst_ids=[DstId(rid=rid, pnc=pid)], dma_engine_mask=sum(1 << e for e in eng),
                                               remote_sem=T.sem["arr%d" % t], src=nw[0],
                                               dst=T.LAND[:, 384 * t + 128 * s:384 * t + 128 * s + 128]))
        g.remote_dma_fused(transfers, local_sem=T.sem["snt%d" % t])
        total["arr%d" % t] = 12
        total["snt%d" % t] = 12
        note("r", {}, [], [("LAND", 384 * t, 384 * t + 384)], "arr%d" % t, 12)

        vts(A("al3"), A("al2"), 512.0, add)
        vcopy(A("l16"), A("psb0", 0, 16))
        if not last:
            vts(A("al4"), A("REF"), float(128 * t), mul)
        vcopy(A("er"), ind(A(FRc, 128, 1536), A("l16", 0, 8)))
        if not last:
            vcopy(A("C", 128 * t, 128 * t + 128), A("a16"))
            vtt(A("alt"), A("al3"), A("NREF"), mul)
        act(A("lamA"), A("psk", 256, 264), AF.Copy)
        vcopy(ind(A(FRc, 0, 1536), A("vo16")), A("er"))
        if not last:
            mms("psb1", [("EF", 0, 2048), ("er", 0, 128)],
                [(T.psb1[:, 384:392], T.EF[:, 128 * r:128 * r + 128], T.er[:, r:128:16], r == 0, r == 15) for r in range(16)])
        vcopy(A("ap16"), A("psk", 256, 264))
        if not last:
            vtt(A("aln"), A("alt"), A("al4"), add)
        for c in range(4 if last else 8):
            act(A("DD", 128 * c, 128 * c + 128), A("psd0", 0, 128), AF.Abs, scale=-1.0, bias=A("lamA", c, c + 1))
        act(A("LE"), ind(A("L", 0, 1024), A("ap16")), AF.Copy, scale=EV)
        act(A(FRn, 640, 1536), ind(A(FRc, 128, 1536), A("FL", 32, 88)), AF.Copy)
        if t > 0:
            act(A(FRn, 128, 128 + 128 * t), ind(A(FRc, 128, 1536), A("FL", 0, 8 * t)), AF.Copy)
        if not last:
            vtt(A("wm"), ind(A(FRc, 128, 1536), A("l16", 8, 16)), A("MK"), mul)
            vtt(A("t0"), A("lamA"), TRc, sub)
            vscan(A("ws"), A("d0S"), A("wm"), mul, add)
            vtt(A("t1"), A("t0"), A("REF"), mul)
            vcopy(A("w16"), A("ws", 15, 128, 16))
            vtt(A("em"), ind(A(FRc, 128, 1536), A("w16")), A("MK"), mul)
            vscan(A("es"), A("d0S"), A("em"), mul, add)
            vtt(A("um"), ind(A("M1"), P), A("u1"), mul)
            vcopy(A("wi"), A("es", 15, 128, 16))
            vts(A("gh"), A("es", 15, 128, 16), 1024.0, ge)
            vts(A("ng"), A("es", 15, 128, 16), 1024.0, lt)
            vts(A("wB"), A("wi"), 1920, band)
            vtt(A("cn"), A("um"), A("af"), add)
            vtt(A("x1"), A("wB"), A("ng"), mul)
            vts(A("cm"), A("cn"), 1023, band)
            vtt(A("ga"), A("gh"), A("aln"), mul)
            vcopy(ind(A("C"), A("v16")), A("cm"))
            vtt(A("gb"), A("ga"), LIc, add)
            vcopy(A("e16"), A("psb1", 384, 392))
        else:
            vtt(A("em"), A("er"), A("MK"), mul)
            vtt(A("t0"), A("lamA"), TRc, sub)
            vscan(A("es"), A("d0S"), A("em"), mul, add)
            vtt(A("t1"), A("t0"), A("REF"), mul)
            vcopy(A("e16"), A("es", 15, 128, 16))
            for c in range(4, 8):
                vts(A("DD", 128 * c, 128 * c + 128), A("psd1", 0, 128), A("lamA", c, c + 1), ne)
            room()
        act(A("fx"), ind(A(FRc, 128, 1536), A("e16")), AF.Copy)
        if t == 0:
            act(A("LO", 0, 1024), A("L", 0, 1024), AF.Copy)
            dma("s", T.lo[0:128:2, :], T.LO[0:128:2, 0:1024], [("LO", 0, 1024)], [], "out0")
        vscan(A("DS"), A("d0D"), A("DD"), add, mn)
        if not last:
            vtt(A("vf"), A("x1"), A("gb"), add)
        vtt(A("t2"), A("DS", 127, 1024, 128), TD, ge)
        if not last:
            vtt(A("vB"), A("x1"), A("ga"), add)
            fix()
        vtt(A("t3"), A("t2"), A("t1"), mul)
        if not last:
            room()
        vtt(A("t4"), A("t3"), TRc, add)
        if not last:
            vcopy(ind(A("Y", 0, 1024), A("v16")), nw)
        vcopy(A("lo16"), A("t4"))
        if not last:
            vcopy(A("v16"), A("vf"))
            vtt(ind(A("L", 0, 1152), A("lo16")), A("LE"), A("ODDN"), add)
            vcopy(A("a16"), ind(A("C"), A("v16")))
            act(A("own"), ind(A("Y", 0, 1024), A("v16")), AF.Copy)
        else:
            vtt(ind(A("LO", 0, 1152), A("lo16")), A("LE"), A("ODDO"), add)
            fix()
            vcopy(ind(A("Y", 0, 1024), A("v16")), nw)
        FRc, FRn = FRn, FRc

    dma("s", T.lo[1:128:2, :], T.LO[1:128:2, 0:1024], [("LO", 0, 1024)], [], "out5")
    dma("s", T.yo[:, 0:512], T.Y[:, 512:1024], [("Y", 512, 1024)], [], "out1")
    dma("s", T.yo[:, 896:1408], T.Y[:, 0:512], [("Y", 0, 512)], [], "out2")
    vts(A("FOt"), A("psm", 0, 88), 512.0, lt, 1408.0, mul)
    vtt(A("FOu"), A("psm", 0, 88), A("FOt"), add)
    vts(A("FO", 0, 56), A("FOu", 32, 88), -512.0, add)
    vts(A("FO", 56, 88), A("FOu", 0, 32), -512.0, add)
    dma("a", T.fo[:, :], T.FO[:, :], [("FO", 0, 88)], [], "out3")
    p = 384 * (RO - 1)
    dma("s", T.yo[:, 512:896], T.LAND[:, p:p + 384], [("LAND", p, p + 384)], [], "out4")
    for sem in ("dv", "ac", "pe", "gp"):
        g.wait_ge(T.sem[sem], count[sem])
    for sem in sorted(total):
        g.wait_ge(T.sem[sem], total[sem])
